import numpy as np
import ml_dtypes


def mxq(x, axis, fmt="e4m3"):
    dtype, down = {"e4m3": (ml_dtypes.float8_e4m3fn, 7), "e5m2": (ml_dtypes.float8_e5m2, 14)}[fmt]
    v = np.moveaxis(np.asarray(x, np.float32).astype(ml_dtypes.bfloat16).astype(np.float64), axis, -1)
    blocks = v.reshape(v.shape[:-1] + (-1, 32))
    amax = np.abs(blocks).max(-1, keepdims=True)
    byte = np.maximum(np.where(amax > 0, np.frexp(amax)[1] - 1 + 127, 0) - down, 1)
    scale = np.exp2(byte - 127.0)
    codes = (blocks / scale).astype(np.float32).astype(dtype).astype(np.float64)
    return np.moveaxis((codes * scale).reshape(v.shape), -1, axis)


WIDE = False


def mx_kscale(k):
    if not WIDE:
        return np.ones(k)
    levels = np.array([10, -10, 5, -5, 0])
    if k % 512:
        return np.exp2(np.random.permutation(np.resize(levels, k // 32))).repeat(32)
    a = np.empty((k // 512, 16))
    for p in range(k // 512):
        a[p, :8] = np.random.permutation(np.resize(levels, 8))
        for g in range(8):
            far = levels[np.abs(levels - a[p, g]) >= 10]
            a[p, g + 8] = far[np.random.randint(len(far))]
    return np.exp2(a.ravel()).repeat(32)


BF16 = ml_dtypes.bfloat16


def bf(x):
    return np.asarray(x, np.float32).astype(BF16)


def f64(x):
    return np.asarray(x).astype(np.float64)


B, J, K, D, F, P = 4, 1024, 512, 512, 512, 128


def ssp(u):
    return np.maximum(u, 0.0) + np.log(0.5 + 0.5 * np.exp(-np.abs(u)))


def draw0():
    s = mx_kscale(K)
    v = mx_kscale(D)
    t = mx_kscale(J)
    r = np.random.uniform(0.05, 0.75, (B, J))
    n = np.arange(K) + 1.0
    basis = np.sqrt(2.0) * np.sin(np.pi * r.reshape(B * J, 1) * n)
    return {"rbf": bf(basis * s),
            "x": bf(np.random.standard_normal((B * J, D)) * v),
            "cut": bf(0.5 * (np.cos(np.pi * r) + 1.0) / t),
            "occ": bf(np.random.uniform(0.5, 1.5, (B, J)) * t),
            "w_f": bf(np.random.standard_normal((K, F)) / np.sqrt(K) / s[:, None]),
            "b_f": bf(0.3 * np.random.standard_normal(F)),
            "w_h": bf(np.random.standard_normal((D, F)) / np.sqrt(D) / v[:, None]),
            "w_a": bf(np.random.standard_normal((D, P)) / np.sqrt(D) / v[:, None]),
            "b_a": bf(0.3 * np.random.standard_normal(P))}


def core(rbf, x, cut, occ, w_f, b_f, w_h, w_a, b_a):
    xq = mxq(f64(x), 1, "e4m3")
    filt = ssp((mxq(f64(rbf), 1, "e4m3") @ mxq(f64(w_f), 0, "e4m3")) + f64(b_f))
    h = xq @ mxq(f64(w_h), 0, "e4m3")
    m = filt * f64(cut).reshape(B * J, 1) * h
    z = (xq @ mxq(f64(w_a), 0, "e4m3")) + f64(b_a)
    e = np.exp(z - z.max(axis=1, keepdims=True))
    a = P * e / e.sum(axis=1, keepdims=True) * f64(occ).reshape(B * J, 1)
    aq = mxq(a.reshape(B, J, P), 1, "e4m3")
    mq = mxq(m.reshape(B, J, F), 1, "e4m3")
    return (aq.swapaxes(1, 2) @ mq) / np.sqrt(J)


def e4m3fn_bytes(y):
    return np.clip(np.asarray(y, np.float64), -448.0, 448.0).astype(np.float32).astype(ml_dtypes.float8_e4m3fn).view(np.uint8)


def e4m3fn_values(b):
    return np.asarray(b, np.uint8).view(ml_dtypes.float8_e4m3fn).astype(np.float64)


def setup_inputs():
    d = draw0()
    x0 = np.asarray(d['x']).astype(np.float64)
    s = (np.max(np.abs(x0), axis=(0,), keepdims=True) / 448.0).astype(np.float32)
    out = {}
    for k, v in d.items():
        if k == 'x':
            out['x_bytes'] = e4m3fn_bytes(x0 / s.astype(np.float64))
            out['x_scale'] = s
        else:
            out[k] = v
    return out


def reference(rbf, x_bytes, x_scale, cut, occ, w_f, b_f, w_h, w_a, b_a):
    return core(rbf, e4m3fn_values(x_bytes) * x_scale.astype(np.float64), cut, occ, w_f, b_f, w_h, w_a, b_a)

@@ -1,0 +1,465 @@
+import math
+from contextlib import ExitStack
+
+import concourse.mybir as mybir
+from concourse.masks import make_identity
+
+B, J, K, D, F, S = 4, 1024, 512, 512, 512, 128
+FLOPS = 2 * B * J * (K * F + D * F + D * S) + 2 * B * S * J * F
+
+F32 = mybir.dt.float32
+BF16 = mybir.dt.bfloat16
+U32 = mybir.dt.uint32
+U8 = mybir.dt.uint8
+FP8 = mybir.dt.float8_e4m3fn
+FP8X4 = mybir.dt.float8_e4m3fn_x4
+ALU = mybir.AluOpType
+ACT = mybir.ActivationFunctionType
+AX = mybir.AxisListType
+
+P = 128
+T = 4
+ROWS = P * T
+NG = B * J // ROWS
+FB = F // P
+SEQ = "B1 R0 T1 T2 q0 Y1 R1 Z0 F0 B2 q1 T3 Y2 M0 R2 R3 v2 F1 B3 Z1 M1 T4 q2 T5 Y3 F2 B4 R4 T6 v3 Z2 M2 q3 F3 Y4 Z3 B5 q4 F4 T7 B6 R5 M3 Y5 v5 Y6 F5 R6 Z4 q5 Z5 B7 F6 v6 Y7 R7 q6 M4 F7 Z6 v7 q7 M5 E0 E1 Z7 M6 E2 E3 E4 E5 W0 E6 M7 E7 W1 W2 H0 W3"
+VEX = [int(e[1]) for e in SEQ.split() if e[0] == "v"]
+LN2 = math.log(2.0)
+TINY = 2.0 ** -64
+
+
+def tile_schnet_slot_cfconv_f5_kernel(
+    tc, rbf, x_bytes, x_scale, cut, occ, w_f, b_f, w_h, w_a, b_a, out
+):
+    nc = tc.nc
+    with ExitStack() as ctx:
+        keep = ctx.enter_context(tc.tile_pool(name="keep", bufs=1))
+        work = ctx.enter_context(tc.tile_pool(name="work", bufs=2))
+        psum = ctx.enter_context(tc.psum_pool(name="psum", bufs=1))
+        ctx.enter_context(tc.manual_schedule())
+
+        rcodes = keep.tile([P, NG * ROWS], U32, name="rcodes", align_bytes=64)
+        rscales = keep.tile([P, NG * ROWS], U8, name="rscales", align_bytes=64)
+        xcodes = keep.tile([P, NG * ROWS], U32, name="xcodes", align_bytes=64)
+        xscales = keep.tile([P, NG * ROWS], U8, name="xscales", align_bytes=64)
+        wfc = keep.tile([P, F], U32, name="wfc", align_bytes=64)
+        wfs = keep.tile([P, F], U8, name="wfs", align_bytes=64)
+        whc = keep.tile([P, F], U32, name="whc", align_bytes=64)
+        whs = keep.tile([P, F], U8, name="whs", align_bytes=64)
+        wac = keep.tile([P, S], U32, name="wac", align_bytes=64)
+        was = keep.tile([P, S], U8, name="was", align_bytes=64)
+        acodes = keep.tile([P, NG * S], U32, name="acodes", align_bytes=64)
+        ascales = keep.tile([P, NG * S], U8, name="ascales", align_bytes=64)
+        sig = keep.tile([P, NG, FB, ROWS], F32, name="sig")
+        zs = keep.tile([P, NG, T, S], F32, name="zs")
+        sc1 = keep.tile([P, D], F32, name="sc1")
+        sc4 = keep.tile([P, T * D], F32, name="sc4")
+        ident = keep.tile([P, P], F32, name="ident")
+        tiny = keep.tile([P, 1], F32, name="tiny")
+        dummy = keep.tile([P, 1], F32, name="dummy")
+        bf_raw = keep.tile([P, FB, 2], BF16, name="bf_raw")
+        nbf = keep.tile([P, FB], F32, name="nbf")
+        cbf = keep.tile([P, FB], F32, name="cbf")
+        ba = keep.tile([P, S], BF16, name="ba")
+        nba = keep.tile([P, S], F32, name="nba")
+        cut_raw = keep.tile([P, NG, T], BF16, name="cut_raw")
+        occ_raw = keep.tile([P, NG, T], BF16, name="occ_raw")
+        ncut = keep.tile([P, NG, T], F32, name="ncut")
+        nmax = keep.tile([P, NG, T], F32, name="nmax")
+        zsum = keep.tile([P, NG, T], F32, name="zsum")
+        rsum = keep.tile([P, NG, T], F32, name="rsum")
+        fac = keep.tile([P, NG, T], F32, name="fac")
+
+        rbf_v = rbf.rearrange("(g m t) k -> g m (t k)", m=P, t=T)
+        xb_v = x_bytes.rearrange("(g m t) k -> g m (t k)", m=P, t=T)
+
+        raw_r = {}
+        raw_x = {}
+
+        def load_x(g):
+            xby = work.tile([P, T * D], U8, name="xby", tag="xby", bufs=4)
+            nc.sync.dma_start(out=xby[:], in_=xb_v[g])
+            raw_x[g] = xby
+
+        def load_r(g):
+            rld = work.tile([P, T * K], BF16, name="rld", tag="rld", bufs=3)
+            nc.sync.dma_start(out=rld[:], in_=rbf_v[g])
+            raw_r[g] = rld
+
+        def load_w(w, cols):
+            wld = work.tile([P, T, cols], BF16, name="wld%d" % cols, tag="wld%d" % cols, bufs=1)
+            nc.sync.dma_start(out=wld[:], in_=w.rearrange("(p j) f -> p j f", j=T))
+            return wld
+
+        nc.scalar.dma_start(out=sc1[:], in_=x_scale.rearrange("o k -> (o k)").partition_broadcast(P))
+        load_x(0)
+        load_r(0)
+        wf_raw = load_w(w_f, F)
+        wa_raw = load_w(w_a, S)
+        load_x(1)
+        load_r(1)
+        load_x(2)
+        load_r(2)
+        with nc.allow_non_contiguous_dma(reason="small vectors"):
+            nc.gpsimd.dma_start(out=bf_raw[:, :, 0], in_=b_f.rearrange("(c p) -> p c", p=P))
+            nc.gpsimd.dma_start(out=ba[:], in_=b_a.partition_broadcast(P))
+            nc.scalar.dma_start(
+                out=occ_raw[:], in_=occ.rearrange("b j -> (b j)").rearrange("(g m t) -> m g t", m=P, t=T)
+            )
+            nc.scalar.dma_start(
+                out=cut_raw[:], in_=cut.rearrange("b j -> (b j)").rearrange("(g m t) -> m g t", m=P, t=T)
+            )
+
+        nc.gpsimd.memset(tiny[:], TINY)
+        make_identity(nc, ident[:])
+        nc.scalar.activation(out=dummy[:], in_=tiny[:], func=ACT.Sigmoid, bias=tiny[:], scale=1.0)
+
+        grp_r = {}
+        grp_x = {}
+        xbf = {}
+
+        def scale_x(g):
+            xb = work.tile([P, T * D], BF16, name="xb", tag="xb", bufs=2)
+            src = raw_x.pop(g)
+            if g == 0:
+                for t in range(T):
+                    cols = slice(t * D, (t + 1) * D)
+                    nc.vector.tensor_tensor(
+                        out=xb[:, cols], in0=src[:, cols].bitcast(FP8), in1=sc1[:], op=ALU.mult
+                    )
+            else:
+                nc.vector.tensor_tensor(out=xb[:], in0=src[:].bitcast(FP8), in1=sc4[:], op=ALU.mult)
+            xbf[g] = xb
+
+        def turn(src, grp_map, g, b):
+            words = src[:].bitcast(F32)
+            bank = psum.tile([P, 2, 2, P], F32, name="tr", tag="tr", bufs=3)
+            for tt in range(2):
+                base = (2 * b + tt) * (K // 2)
+                for u in range(2):
+                    nc.tensor.transpose(bank[:, tt, u, :], words[:, base + u : base + K // 2 : 2], ident[:])
+            return bank
+
+        def turn_out(bank, grp, b, on_vector):
+            dst = grp[:].bitcast(F32)[:, b * 512 : (b + 1) * 512].rearrange("p (t r u) -> p t r u", t=2, u=2)
+            src = bank[:].rearrange("p t u r -> p t r u")
+            if on_vector:
+                nc.vector.tensor_copy(out=dst, in_=src)
+            else:
+                nc.scalar.copy(out=dst, in_=src)
+
+        pend = {}
+
+        def turn_all(src, grp_map, g, late=False):
+            grp = work.tile([P, ROWS * T], BF16, name="grp", tag="grp", bufs=4, align_bytes=64)
+            for b in range(2):
+                bank = turn(src, grp_map, g, b)
+                if late and b == 1:
+                    pend[g] = (bank, grp)
+                else:
+                    turn_out(bank, grp, b, False)
+            grp_map[g] = grp
+
+        def turn_late(g):
+            bank, grp = pend.pop(g)
+            turn_out(bank, grp, 1, True)
+
+        def quant(grp, codes, scales):
+            nc.vector.quantize_mx(out=codes.bitcast(FP8X4), scales=scales, in_=grp)
+
+        def mm(o, lc, ls, lcols, rc, rs, rcols, start=True, stop=True):
+            nc.tensor.matmul_mx(
+                out=o,
+                lhsT=lc[:, lcols].bitcast(FP8X4),
+                lhsT_scale=ls[:, lcols],
+                rhs=rc[:, rcols].bitcast(FP8X4),
+                rhs_scale=rs[:, rcols],
+                start=start,
+                stop=stop,
+            )
+
+        def gcols(g):
+            return slice(g * ROWS, (g + 1) * ROWS)
+
+        def filt_mm(g, fb):
+            bank = psum.tile([P, ROWS], F32, name="fps", tag="fps", bufs=2)
+            mm(bank[:], wfc, wfs, slice(fb * P, (fb + 1) * P), rcodes, rscales, gcols(g))
+            return bank
+
+        def sig_act(g, fb, bank):
+            nc.scalar.activation(
+                out=sig[:, g, fb, :], in_=bank[:], func=ACT.Sigmoid, bias=nbf[:, fb : fb + 1], scale=1.0
+            )
+
+        def slot_mm(g):
+            bank = psum.tile([P, T, S], F32, name="hps", tag="hps", bufs=2)
+            for t in range(T):
+                c0 = g * ROWS + t * P
+                mm(bank[:, t, :], xcodes, xscales, slice(c0, c0 + P), wac, was, slice(0, S))
+            return bank
+
+        zbank = {}
+
+        def slot_bias(g):
+            nc.vector.tensor_tensor(
+                out=zs[:, g, :, :],
+                in0=zbank.pop(g)[:],
+                in1=nba[:].unsqueeze(1).to_broadcast([P, T, S]),
+                op=ALU.add,
+            )
+
+        def slot_max(g):
+            nc.vector.tensor_reduce(out=nmax[:, g, :], in_=zs[:, g, :, :], axis=AX.X, op=ALU.min)
+
+        scale_x(0)
+        turn_all(raw_r.pop(0), grp_r, 0)
+        wf_grp = work.tile([P, F * T], BF16, name="wgrp", tag="wgrp", bufs=1, align_bytes=64)
+        nc.vector.tensor_scalar(
+            out=wf_grp[:].rearrange("p (f j) -> p f j", j=T),
+            in0=wf_raw[:].rearrange("p j f -> p f j"),
+            scalar1=-1.0,
+            scalar2=None,
+            op0=ALU.mult,
+        )
+        for t in range(T):
+            nc.gpsimd.tensor_scalar(
+                out=sc4[:, t * D : (t + 1) * D], in0=sc1[:], scalar1=1.0, scalar2=0.0, op0=ALU.mult, op1=ALU.add
+            )
+        nc.gpsimd.tensor_scalar(
+            out=nbf[:], in0=bf_raw[:, :, 0], scalar1=-1.0, scalar2=None, op0=ALU.mult
+        )
+        nc.gpsimd.tensor_scalar(
+            out=cbf[:], in0=nbf[:], scalar1=LN2, scalar2=None, op0=ALU.add
+        )
+        turn_all(xbf.pop(0), grp_x, 0)
+        quant(wf_grp[:], wfc[:], wfs[:])
+        wa_grp = work.tile([P, S * T], BF16, name="wagrp", tag="wagrp", bufs=1, align_bytes=64)
+        nc.vector.tensor_scalar(
+            out=wa_grp[:].rearrange("p (f j) -> p f j", j=T),
+            in0=wa_raw[:].rearrange("p j f -> p f j"),
+            scalar1=-1.0,
+            scalar2=None,
+            op0=ALU.mult,
+        )
+        nc.gpsimd.tensor_scalar(out=nba[:], in0=ba[:], scalar1=-1.0, scalar2=None, op0=ALU.mult)
+        nc.gpsimd.tensor_scalar(out=ncut[:], in0=cut_raw[:], scalar1=-1.0, scalar2=None, op0=ALU.mult)
+        quant(wa_grp[:], wac[:], was[:])
+
+        at = {}
+
+        def slot_exp(g):
+            for t in range(T):
+                nc.scalar.activation(
+                    out=zs[:, g, t, :],
+                    in_=zs[:, g, t, :],
+                    func=ACT.Exp,
+                    bias=nmax[:, g, t : t + 1],
+                    scale=-1.0,
+                    accum_out=zsum[:, g, t : t + 1],
+                )
+
+        def slot_weights(g0, n):
+            gs = slice(g0, g0 + n)
+            nc.vector.reciprocal(out=rsum[:, gs, :], in_=zsum[:, gs, :])
+            nc.vector.scalar_tensor_tensor(
+                out=fac[:, gs, :], in0=rsum[:, gs, :], scalar=float(S), in1=occ_raw[:, gs, :], op0=ALU.mult, op1=ALU.mult
+            )
+            for g in range(g0, g0 + n):
+                if g % 4 == 0:
+                    at[g // 4] = work.tile([P, 4, S, T], BF16, name="grp", tag="grp", bufs=4, align_bytes=64)
+                nc.gpsimd.tensor_tensor(
+                    out=at[g // 4][:, g % 4, :, :],
+                    in0=zs[:, g, :, :].rearrange("p t n -> p n t"),
+                    in1=fac[:, g, :].unsqueeze(1).to_broadcast([P, S, T]),
+                    op=ALU.mult,
+                )
+
+        pend_r = {}
+
+        def ev_R(s):
+            if s + 3 < NG:
+                load_r(s + 3)
+            quant(grp_r.pop(s)[:], rcodes[:, gcols(s)], rscales[:, gcols(s)])
+
+        def ev_T(s):
+            turn_all(raw_r.pop(s), grp_r, s, False)
+
+        def ev_F(s):
+            for fb in range(FB):
+                sig_act(s, fb, filt_mm(s, fb))
+
+        def ev_Z(k):
+            zbank[k] = slot_mm(k)
+
+        def ev_M(k):
+            slot_bias(k)
+            slot_max(k)
+
+        def ev_Y(k):
+            turn_all(xbf.pop(k), grp_x, k, k in VEX)
+
+        def ev_q(k):
+            quant(grp_x.pop(k)[:], xcodes[:, gcols(k)], xscales[:, gcols(k)])
+
+        def ev_B(k):
+            if k + 2 < NG:
+                load_x(k + 2)
+            if k == 3:
+                wh[0] = load_w(w_h, F)
+            scale_x(k)
+
+        def ev_H(k):
+            wh_grp = work.tile([P, F * T], BF16, name="wgrp", tag="wgrp", bufs=1, align_bytes=64)
+            nc.vector.tensor_copy(
+                out=wh_grp[:].rearrange("p (f j) -> p f j", j=T), in_=wh[0][:].rearrange("p j f -> p f j")
+            )
+            quant(wh_grp[:], whc[:], whs[:])
+
+        def ev_W(k):
+            slot_weights(2 * k, 2)
+
+        wh = {}
+        events = {
+            "R": ev_R, "T": ev_T, "F": ev_F, "Z": ev_Z, "M": ev_M, "Y": ev_Y, "q": ev_q, "B": ev_B,
+            "E": slot_exp, "W": ev_W, "H": ev_H, "v": turn_late,
+        }
+        for ev in SEQ.split():
+            events[ev[0]](int(ev[1]))
+
+        def quant_a(h):
+            cols = slice(h * 4 * S, (h + 1) * 4 * S)
+            quant(at[h][:].rearrange("p g n t -> p (g n t)"), acodes[:, cols], ascales[:, cols])
+
+        def log_act(g, lo, hi):
+            nc.scalar.activation(
+                out=sig[:, g, lo:hi, :], in_=sig[:, g, lo:hi, :], func=ACT.Ln, bias=tiny[:], scale=2.0
+            )
+
+        spt = {}
+        spc = {}
+        mt = {}
+        fbank = {}
+        hbank = {}
+        ybank = {}
+        mcodes = {}
+        NQ = NG * FB
+
+        def h_mm(i):
+            g, q = divmod(i, FB)
+            hbank[i] = psum.tile([P, T, P], F32, name="hps", tag="hps", bufs=2)
+            for t in range(T):
+                c0 = g * ROWS + t * P
+                mm(hbank[i][:, t, :], xcodes, xscales, slice(c0, c0 + P), whc, whs, slice(q * P, (q + 1) * P))
+
+        def f_mm(i):
+            g, q = divmod(i, FB)
+            fbank[i] = filt_mm(g, q)
+
+        def min_op(i):
+            g, q = divmod(i, FB)
+            if q == 0:
+                spt[g] = work.tile([P, FB, ROWS], F32, name="spt", tag="spt", bufs=2)
+            nc.vector.scalar_tensor_tensor(
+                out=spt[g][:, q, :],
+                in0=fbank.pop(i)[:],
+                scalar=cbf[:, q : q + 1],
+                in1=sig[:, g, q, :],
+                op0=ALU.add,
+                op1=ALU.min,
+            )
+
+        def back(i):
+            g, q = divmod(i, FB)
+            if q == 0:
+                spc[g] = work.tile([P, T, F], F32, name="spc", tag="spc", bufs=2)
+            bank = psum.tile([P, F], F32, name="tr", tag="tr", bufs=3)
+            for fb in range(FB):
+                nc.tensor.transpose(
+                    bank[:, fb * P : (fb + 1) * P], spt[g][:, fb, q * P : (q + 1) * P], ident[:]
+                )
+            nc.scalar.activation(
+                out=spc[g][:, q, :], in_=bank[:], func=ACT.Copy, scale=ncut[:, g, q : q + 1]
+            )
+
+        def mul_op(i):
+            g, q = divmod(i, FB)
+            if q == 0:
+                mt[g] = work.tile([P, F * T], BF16, name="grp", tag="grp", bufs=4, align_bytes=64)
+            nc.vector.tensor_tensor(
+                out=mt[g][:, q * 512 : (q + 1) * 512].rearrange("p (f t) -> p f t", t=T),
+                in0=hbank.pop(i)[:].rearrange("p t f -> p f t"),
+                in1=spc[g][:, :, q * P : (q + 1) * P].rearrange("p t f -> p f t"),
+                op=ALU.mult,
+            )
+
+        def quant_m(g, lo, hi):
+            if lo == 0:
+                mcodes[g] = (
+                    work.tile([P, F], U32, name="mc", tag="mc", bufs=2, align_bytes=64),
+                    work.tile([P, F], U8, name="ms", tag="ms", bufs=2, align_bytes=64),
+                )
+            mc, ms = mcodes[g]
+            quant(mt[g][:, lo * T : hi * T], mc[:, lo:hi], ms[:, lo:hi])
+
+        def y_mm(g, lo, hi):
+            b, half = divmod(g, 2)
+            if half == 0:
+                if lo == 0:
+                    ybank[b, lo] = psum.tile([P, F], F32, name="yps", tag="yps", bufs=1)
+                else:
+                    ybank[b, lo] = psum.tile([P, F], F32, name="fps", tag="fps", bufs=2)
+            mc, ms = mcodes[g]
+            mm(
+                ybank[b, lo][:, : hi - lo], acodes, ascales, slice(g * S, (g + 1) * S), mc, ms, slice(lo, hi),
+                start=(half == 0), stop=(half == 1),
+            )
+
+        def y_out(b, lo, hi):
+            yo = work.tile([P, F], F32, name="yo", tag="yo", bufs=2)
+            nc.scalar.activation(
+                out=yo[:, : hi - lo], in_=ybank[b, lo][:, : hi - lo], func=ACT.Copy, scale=1.0 / math.sqrt(J)
+            )
+            nc.sync.dma_start(out=out[b][:, lo:hi], in_=yo[:, : hi - lo])
+
+        log_act(0, 0, 2)
+        log_act(0, 2, 4)
+        f_mm(0)
+        f_mm(1)
+        for i in range(NQ + 12):
+            g, q = divmod(i, FB)
+            if q % 2 == 0 and g + 1 < NG:
+                log_act(g + 1, q, q + 2)
+            if i < NQ:
+                if i >= 4:
+                    back(i - 4)
+                min_op(i)
+            elif i < NQ + 2:
+                back(2 * i - NQ - 4)
+                back(2 * i - NQ - 3)
+            if i == 3:
+                quant_a(0)
+            if i == 7:
+                quant_a(1)
+            if q == 0 and 0 <= g - 3 < NG - 1:
+                quant_m(g - 3, 0, F)
+            if 0 <= i - 8 < NQ:
+                mul_op(i - 8)
+            if i + 2 < NQ:
+                f_mm(i + 2)
+            if 0 <= i - 6 < NQ:
+                h_mm(i - 6)
+            if q == 1 and 0 <= g - 3 < NG - 2:
+                y_mm(g - 3, 0, F)
+            if q == 1 and g - 3 == NG - 2:
+                y_mm(g - 3, 0, F // 2)
+                y_mm(g - 3, F // 2, F)
+            if q == 3 and 0 <= g - 3 < NG - 1 and (g - 3) % 2 == 1:
+                y_out((g - 3) // 2, 0, F)
+            if i - 8 == NQ - 2:
+                quant_m(NG - 1, 0, F // 2)
+                y_mm(NG - 1, 0, F // 2)
+                y_out(B - 1, 0, F // 2)
+            if i - 8 == NQ - 1:
+                quant_m(NG - 1, F // 2, F)
+                y_mm(NG - 1, F // 2, F)
+                y_out(B - 1, F // 2, F)

@@ -22,8 +22,9 @@ T = 4
 ROWS = P * T
 NG = B * J // ROWS
 FB = F // P
-SEQ = "B1 R0 T1 T2 q0 Y1 R1 Z0 F0 B2 q1 T3 Y2 M0 R2 R3 v2 F1 B3 Z1 M1 T4 q2 T5 Y3 F2 B4 R4 T6 v3 Z2 M2 q3 F3 Y4 Z3 B5 q4 F4 T7 B6 R5 M3 Y5 v5 Y6 F5 R6 Z4 q5 Z5 B7 F6 v6 Y7 R7 q6 M4 F7 Z6 v7 q7 M5 E0 E1 Z7 M6 E2 E3 E4 E5 W0 E6 M7 E7 W1 W2 H0 W3"
-VEX = [int(e[1]) for e in SEQ.split() if e[0] == "v"]
+VEX = []
+LEAD, NUM, DEN, E0, EN, ED = 2, 4, 3, 11, 3, 2
+AFV = (4, 5, 6, 7)
 LN2 = math.log(2.0)
 TINY = 2.0 ** -64
 
@@ -52,15 +53,16 @@ def tile_schnet_slot_cfconv_f5_kernel(
         ascales = keep.tile([P, NG * S], U8, name="ascales", align_bytes=64)
         sig = keep.tile([P, NG, FB, ROWS], F32, name="sig")
         zs = keep.tile([P, NG, T, S], F32, name="zs")
-        sc1 = keep.tile([P, D], F32, name="sc1")
         sc4 = keep.tile([P, T * D], F32, name="sc4")
         ident = keep.tile([P, P], F32, name="ident")
         tiny = keep.tile([P, 1], F32, name="tiny")
         dummy = keep.tile([P, 1], F32, name="dummy")
-        bf_raw = keep.tile([P, FB, 2], BF16, name="bf_raw")
-        nbf = keep.tile([P, FB], F32, name="nbf")
+        srow = keep.tile([P, P], F32, name="srow")
+        brow = keep.tile([P, P], BF16, name="brow")
+        brow32 = keep.tile([P, P], F32, name="brow32")
+        sccol = keep.tile([P, FB], F32, name="sccol")
+        nbf = keep.tile([P, FB + 1], F32, name="nbf")
         cbf = keep.tile([P, FB], F32, name="cbf")
-        ba = keep.tile([P, S], BF16, name="ba")
         nba = keep.tile([P, S], F32, name="nba")
         cut_raw = keep.tile([P, NG, T], BF16, name="cut_raw")
         occ_raw = keep.tile([P, NG, T], BF16, name="occ_raw")
@@ -82,7 +84,7 @@ def tile_schnet_slot_cfconv_f5_kernel(
             raw_x[g] = xby
 
         def load_r(g):
-            rld = work.tile([P, T * K], BF16, name="rld", tag="rld", bufs=3)
+            rld = work.tile([P, T * K], BF16, name="rld", tag="rld", bufs=2, align_bytes=64)
             nc.sync.dma_start(out=rld[:], in_=rbf_v[g])
             raw_r[g] = rld
 
@@ -91,24 +93,19 @@ def tile_schnet_slot_cfconv_f5_kernel(
             nc.sync.dma_start(out=wld[:], in_=w.rearrange("(p j) f -> p j f", j=T))
             return wld
 
-        nc.scalar.dma_start(out=sc1[:], in_=x_scale.rearrange("o k -> (o k)").partition_broadcast(P))
-        load_x(0)
+        nc.gpsimd.memset(srow[:], 0.0)
+        nc.gpsimd.memset(brow[:], 0.0)
+        nc.sync.dma_start(out=srow[0:FB, :], in_=x_scale.rearrange("o (c p) -> (o c) p", p=P))
+        nc.scalar.dma_start(out=brow[0:FB, :], in_=b_f.rearrange("(c p) -> c p", p=P))
+        nc.scalar.dma_start(out=brow[FB : FB + 1, :], in_=b_a.rearrange("(c p) -> c p", p=P))
         load_r(0)
         wf_raw = load_w(w_f, F)
+        load_x(0)
+        load_r(1)
         wa_raw = load_w(w_a, S)
         load_x(1)
-        load_r(1)
         load_x(2)
         load_r(2)
-        with nc.allow_non_contiguous_dma(reason="small vectors"):
-            nc.gpsimd.dma_start(out=bf_raw[:, :, 0], in_=b_f.rearrange("(c p) -> p c", p=P))
-            nc.gpsimd.dma_start(out=ba[:], in_=b_a.partition_broadcast(P))
-            nc.scalar.dma_start(
-                out=occ_raw[:], in_=occ.rearrange("b j -> (b j)").rearrange("(g m t) -> m g t", m=P, t=T)
-            )
-            nc.scalar.dma_start(
-                out=cut_raw[:], in_=cut.rearrange("b j -> (b j)").rearrange("(g m t) -> m g t", m=P, t=T)
-            )
 
         nc.gpsimd.memset(tiny[:], TINY)
         make_identity(nc, ident[:])
@@ -119,13 +116,13 @@ def tile_schnet_slot_cfconv_f5_kernel(
         xbf = {}
 
         def scale_x(g):
-            xb = work.tile([P, T * D], BF16, name="xb", tag="xb", bufs=2)
+            xb = work.tile([P, T * D], BF16, name="xb", tag="xb", bufs=3, align_bytes=64)
             src = raw_x.pop(g)
             if g == 0:
                 for t in range(T):
                     cols = slice(t * D, (t + 1) * D)
                     nc.vector.tensor_tensor(
-                        out=xb[:, cols], in0=src[:, cols].bitcast(FP8), in1=sc1[:], op=ALU.mult
+                        out=xb[:, cols], in0=src[:, cols].bitcast(FP8), in1=sc4[:, 0:D], op=ALU.mult
                     )
             else:
                 nc.vector.tensor_tensor(out=xb[:], in0=src[:].bitcast(FP8), in1=sc4[:], op=ALU.mult)
@@ -133,7 +130,7 @@ def tile_schnet_slot_cfconv_f5_kernel(
 
         def turn(src, grp_map, g, b):
             words = src[:].bitcast(F32)
-            bank = psum.tile([P, 2, 2, P], F32, name="tr", tag="tr", bufs=3)
+            bank = psum.tile([P, 2, 2, P], F32, name="tr", tag="bank", bufs=8)
             for tt in range(2):
                 base = (2 * b + tt) * (K // 2)
                 for u in range(2):
@@ -182,7 +179,7 @@ def tile_schnet_slot_cfconv_f5_kernel(
             return slice(g * ROWS, (g + 1) * ROWS)
 
         def filt_mm(g, fb):
-            bank = psum.tile([P, ROWS], F32, name="fps", tag="fps", bufs=2)
+            bank = psum.tile([P, ROWS], F32, name="fps", tag="bank", bufs=8)
             mm(bank[:], wfc, wfs, slice(fb * P, (fb + 1) * P), rcodes, rscales, gcols(g))
             return bank
 
@@ -192,7 +189,7 @@ def tile_schnet_slot_cfconv_f5_kernel(
             )
 
         def slot_mm(g):
-            bank = psum.tile([P, T, S], F32, name="hps", tag="hps", bufs=2)
+            bank = psum.tile([P, T, S], F32, name="hps", tag="bank", bufs=8)
             for t in range(T):
                 c0 = g * ROWS + t * P
                 mm(bank[:, t, :], xcodes, xscales, slice(c0, c0 + P), wac, was, slice(0, S))
@@ -211,9 +208,16 @@ def tile_schnet_slot_cfconv_f5_kernel(
         def slot_max(g):
             nc.vector.tensor_reduce(out=nmax[:, g, :], in_=zs[:, g, :, :], axis=AX.X, op=ALU.min)
 
-        scale_x(0)
-        turn_all(raw_r.pop(0), grp_r, 0)
+        nc.gpsimd.tensor_scalar(out=brow32[:], in0=brow[:], scalar1=-1.0, scalar2=None, op0=ALU.mult)
         wf_grp = work.tile([P, F * T], BF16, name="wgrp", tag="wgrp", bufs=1, align_bytes=64)
+        rowbank = psum.tile([P, P], F32, name="hps", tag="bank", bufs=8)
+        nc.tensor.transpose(rowbank[:], srow[:], ident[:])
+        nc.scalar.copy(out=sccol[:], in_=rowbank[:, :FB])
+        grp_r[0] = work.tile([P, ROWS * T], BF16, name="grp", tag="grp", bufs=4, align_bytes=64)
+        rb0 = turn(raw_r[0], None, 0, 0)
+        rb1 = turn(raw_r[0], None, 0, 1)
+        turn_out(rb0, grp_r[0], 0, False)
+        turn_out(rb1, grp_r[0], 1, True)
         nc.vector.tensor_scalar(
             out=wf_grp[:].rearrange("p (f j) -> p f j", j=T),
             in0=wf_raw[:].rearrange("p j f -> p f j"),
@@ -221,31 +225,24 @@ def tile_schnet_slot_cfconv_f5_kernel(
             scalar2=None,
             op0=ALU.mult,
         )
-        for t in range(T):
-            nc.gpsimd.tensor_scalar(
-                out=sc4[:, t * D : (t + 1) * D], in0=sc1[:], scalar1=1.0, scalar2=0.0, op0=ALU.mult, op1=ALU.add
-            )
-        nc.gpsimd.tensor_scalar(
-            out=nbf[:], in0=bf_raw[:, :, 0], scalar1=-1.0, scalar2=None, op0=ALU.mult
-        )
-        nc.gpsimd.tensor_scalar(
-            out=cbf[:], in0=nbf[:], scalar1=LN2, scalar2=None, op0=ALU.add
-        )
-        turn_all(xbf.pop(0), grp_x, 0)
+        scbank = psum.tile([P, FB, P], F32, name="hps", tag="bank", bufs=8)
+        for c in range(FB):
+            nc.tensor.transpose(scbank[:, c, :], sccol[:, c : c + 1].to_broadcast([P, P]), ident[:])
+        nc.scalar.copy(out=sc4[:, 0:D], in_=scbank[:].rearrange("p c q -> p (c q)"))
+        quant(grp_r[0][:], rcodes[:, gcols(0)], rscales[:, gcols(0)])
         quant(wf_grp[:], wfc[:], wfs[:])
-        wa_grp = work.tile([P, S * T], BF16, name="wagrp", tag="wagrp", bufs=1, align_bytes=64)
-        nc.vector.tensor_scalar(
-            out=wa_grp[:].rearrange("p (f j) -> p f j", j=T),
-            in0=wa_raw[:].rearrange("p j f -> p f j"),
-            scalar1=-1.0,
-            scalar2=None,
-            op0=ALU.mult,
-        )
-        nc.gpsimd.tensor_scalar(out=nba[:], in0=ba[:], scalar1=-1.0, scalar2=None, op0=ALU.mult)
-        nc.gpsimd.tensor_scalar(out=ncut[:], in0=cut_raw[:], scalar1=-1.0, scalar2=None, op0=ALU.mult)
-        quant(wa_grp[:], wac[:], was[:])
+        rowbank2 = psum.tile([P, P], F32, name="hps", tag="bank", bufs=8)
+        nc.tensor.transpose(rowbank2[:], brow32[:], ident[:])
+        nc.scalar.copy(out=nbf[:], in_=rowbank2[:, : FB + 1])
+        nc.gpsimd.tensor_scalar(out=cbf[:], in0=nbf[:, :FB], scalar1=LN2, scalar2=None, op0=ALU.add)
+        scale_x(0)
+        for t in range(1, T):
+            nc.scalar.copy(out=sc4[:, t * D : (t + 1) * D], in_=scbank[:].rearrange("p c q -> p (c q)"))
+        babank = psum.tile([P, S], F32, name="hps", tag="bank", bufs=8)
+        nc.tensor.transpose(babank[:], nbf[:, FB : FB + 1].to_broadcast([P, P]), ident[:])
 
         at = {}
+        wh = {}
 
         def slot_exp(g):
             for t in range(T):
@@ -266,65 +263,89 @@ def tile_schnet_slot_cfconv_f5_kernel(
             )
             for g in range(g0, g0 + n):
                 if g % 4 == 0:
-                    at[g // 4] = work.tile([P, 4, S, T], BF16, name="grp", tag="grp", bufs=4, align_bytes=64)
-                nc.gpsimd.tensor_tensor(
+                    at[g // 4] = work.tile([P, 4, S, T], BF16, name="at", tag="xb", bufs=3, align_bytes=64)
+                (nc.vector if g in AFV else nc.gpsimd).tensor_tensor(
                     out=at[g // 4][:, g % 4, :, :],
                     in0=zs[:, g, :, :].rearrange("p t n -> p n t"),
                     in1=fac[:, g, :].unsqueeze(1).to_broadcast([P, S, T]),
                     op=ALU.mult,
                 )
 
-        pend_r = {}
+        bank_r = {}
 
-        def ev_R(s):
+        def turn_r(n):
+            grp_r[n] = work.tile([P, ROWS * T], BF16, name="grp", tag="grp", bufs=4, align_bytes=64)
+            bank_r[n] = (turn(raw_r[n], None, n, 0), turn(raw_r[n], None, n, 1))
+            turn_out(bank_r[n][0], grp_r[n], 0, False)
+            if (n, 1) not in VEX:
+                turn_out(bank_r[n][1], grp_r[n], 1, False)
+
+        def quant_r(n):
+            if (n, 1) in VEX:
+                turn_out(bank_r[n][1], grp_r[n], 1, True)
+            quant(grp_r.pop(n)[:], rcodes[:, gcols(n)], rscales[:, gcols(n)])
+
+        for s in range(NG + 1):
             if s + 3 < NG:
                 load_r(s + 3)
-            quant(grp_r.pop(s)[:], rcodes[:, gcols(s)], rscales[:, gcols(s)])
-
-        def ev_T(s):
-            turn_all(raw_r.pop(s), grp_r, s, False)
-
-        def ev_F(s):
-            for fb in range(FB):
-                sig_act(s, fb, filt_mm(s, fb))
-
-        def ev_Z(k):
-            zbank[k] = slot_mm(k)
-
-        def ev_M(k):
-            slot_bias(k)
-            slot_max(k)
-
-        def ev_Y(k):
-            turn_all(xbf.pop(k), grp_x, k, k in VEX)
-
-        def ev_q(k):
-            quant(grp_x.pop(k)[:], xcodes[:, gcols(k)], xscales[:, gcols(k)])
-
-        def ev_B(k):
-            if k + 2 < NG:
-                load_x(k + 2)
-            if k == 3:
+                load_x(s + 3)
+            if s == 2:
                 wh[0] = load_w(w_h, F)
-            scale_x(k)
-
-        def ev_H(k):
-            wh_grp = work.tile([P, F * T], BF16, name="wgrp", tag="wgrp", bufs=1, align_bytes=64)
-            nc.vector.tensor_copy(
-                out=wh_grp[:].rearrange("p (f j) -> p f j", j=T), in_=wh[0][:].rearrange("p j f -> p f j")
-            )
-            quant(wh_grp[:], whc[:], whs[:])
-
-        def ev_W(k):
-            slot_weights(2 * k, 2)
-
-        wh = {}
-        events = {
-            "R": ev_R, "T": ev_T, "F": ev_F, "Z": ev_Z, "M": ev_M, "Y": ev_Y, "q": ev_q, "B": ev_B,
-            "E": slot_exp, "W": ev_W, "H": ev_H, "v": turn_late,
-        }
-        for ev in SEQ.split():
-            events[ev[0]](int(ev[1]))
+            if s == 5:
+                nc.sync.dma_start(
+                    out=occ_raw[:], in_=occ.rearrange("b j -> (b j)").rearrange("(g m t) -> m g t", m=P, t=T)
+                )
+                nc.sync.dma_start(
+                    out=cut_raw[:], in_=cut.rearrange("b j -> (b j)").rearrange("(g m t) -> m g t", m=P, t=T)
+                )
+                nc.gpsimd.tensor_scalar(out=ncut[:], in0=cut_raw[:], scalar1=-1.0, scalar2=None, op0=ALU.mult)
+            if s < NG:
+                for fb in range(FB):
+                    sig_act(s, fb, filt_mm(s, fb))
+            if s == 0:
+                turn_r(1)
+                wa_grp = work.tile([P, S * T], BF16, name="wagrp", tag="wagrp", bufs=1, align_bytes=64)
+                nc.vector.tensor_scalar(
+                    out=wa_grp[:].rearrange("p (f j) -> p f j", j=T),
+                    in0=wa_raw[:].rearrange("p j f -> p f j"),
+                    scalar1=-1.0,
+                    scalar2=None,
+                    op0=ALU.mult,
+                )
+            if s > 0:
+                quant(grp_x.pop(s - 1)[:], xcodes[:, gcols(s - 1)], xscales[:, gcols(s - 1)])
+                zbank[s - 1] = slot_mm(s - 1)
+            if s > 1:
+                slot_max(s - 2)
+            if s < NG:
+                grp_x[s] = work.tile([P, ROWS * T], BF16, name="grp", tag="grp", bufs=4, align_bytes=64)
+                bank2 = turn(xbf[s], None, s, 0)
+                bank3 = turn(xbf[s], None, s, 1)
+                turn_out(bank2, grp_x[s], 0, False)
+                if (s, 3) not in VEX:
+                    turn_out(bank3, grp_x[s], 1, False)
+            if s == 0:
+                quant_r(1)
+                quant(wa_grp[:], wac[:], was[:])
+                nc.vector.tensor_copy(out=nba[:], in_=babank[:])
+            if s + 2 < NG:
+                turn_r(s + 2)
+            if s + 1 < NG:
+                scale_x(s + 1)
+            if s > 0:
+                slot_bias(s - 1)
+            if s < NG and (s, 3) in VEX:
+                turn_out(bank3, grp_x[s], 1, True)
+            if s + 2 < NG:
+                quant_r(s + 2)
+            if s == 7:
+                wh[1] = work.tile([P, F * T], BF16, name="wgrp", tag="wgrp", bufs=1, align_bytes=64)
+                nc.vector.tensor_copy(
+                    out=wh[1][:].rearrange("p (f j) -> p f j", j=T), in_=wh[0][:].rearrange("p j f -> p f j")
+                )
+            if s == 8:
+                quant(wh[1][:], whc[:], whs[:])
+        slot_max(NG - 1)
 
         def quant_a(h):
             cols = slice(h * 4 * S, (h + 1) * 4 * S)
@@ -346,7 +367,7 @@ def tile_schnet_slot_cfconv_f5_kernel(
 
         def h_mm(i):
             g, q = divmod(i, FB)
-            hbank[i] = psum.tile([P, T, P], F32, name="hps", tag="hps", bufs=2)
+            hbank[i] = psum.tile([P, T, P], F32, name="hps", tag="bank", bufs=8)
             for t in range(T):
                 c0 = g * ROWS + t * P
                 mm(hbank[i][:, t, :], xcodes, xscales, slice(c0, c0 + P), whc, whs, slice(q * P, (q + 1) * P))
@@ -368,18 +389,21 @@ def tile_schnet_slot_cfconv_f5_kernel(
                 op1=ALU.min,
             )
 
-        def back(i):
-            g, q = divmod(i, FB)
-            if q == 0:
+        def back(i, n):
+            g, q0 = divmod(i, FB)
+            if q0 == 0:
                 spc[g] = work.tile([P, T, F], F32, name="spc", tag="spc", bufs=2)
-            bank = psum.tile([P, F], F32, name="tr", tag="tr", bufs=3)
-            for fb in range(FB):
-                nc.tensor.transpose(
-                    bank[:, fb * P : (fb + 1) * P], spt[g][:, fb, q * P : (q + 1) * P], ident[:]
+            banks = {}
+            for q in range(q0, q0 + n):
+                banks[q] = psum.tile([P, F], F32, name="tr", tag="bank", bufs=8)
+                for fb in range(FB):
+                    nc.tensor.transpose(
+                        banks[q][:, fb * P : (fb + 1) * P], spt[g][:, fb, q * P : (q + 1) * P], ident[:]
+                    )
+            for q in range(q0, q0 + n):
+                nc.scalar.activation(
+                    out=spc[g][:, q, :], in_=banks[q][:], func=ACT.Copy, scale=ncut[:, g, q : q + 1]
                 )
-            nc.scalar.activation(
-                out=spc[g][:, q, :], in_=bank[:], func=ACT.Copy, scale=ncut[:, g, q : q + 1]
-            )
 
         def mul_op(i):
             g, q = divmod(i, FB)
@@ -393,29 +417,33 @@ def tile_schnet_slot_cfconv_f5_kernel(
             )
 
         def quant_m(g, lo, hi):
-            if lo == 0:
-                mcodes[g] = (
-                    work.tile([P, F], U32, name="mc", tag="mc", bufs=2, align_bytes=64),
-                    work.tile([P, F], U8, name="ms", tag="ms", bufs=2, align_bytes=64),
+            b, half = divmod(g, 2)
+            if half == 0:
+                tag, bufs = (("rld", 2), ("rld", 2), ("xb", 3), ("wgrp", 1))[b]
+                mcodes[b] = (
+                    work.tile([P, 2 * F], U32, name="mc" + tag, tag=tag, bufs=bufs, align_bytes=64),
+                    work.tile([P, 2 * F], U8, name="ms", tag="ms", bufs=4, align_bytes=64),
                 )
-            mc, ms = mcodes[g]
-            quant(mt[g][:, lo * T : hi * T], mc[:, lo:hi], ms[:, lo:hi])
+            mc, ms = mcodes[b]
+            cols = slice(half * F + lo, half * F + hi)
+            quant(mt[g][:, lo * T : hi * T], mc[:, cols], ms[:, cols])
 
         def y_mm(g, lo, hi):
             b, half = divmod(g, 2)
             if half == 0:
                 if lo == 0:
-                    ybank[b, lo] = psum.tile([P, F], F32, name="yps", tag="yps", bufs=1)
+                    ybank[b, lo] = psum.tile([P, F], F32, name="hps", tag="bank", bufs=8)
                 else:
-                    ybank[b, lo] = psum.tile([P, F], F32, name="fps", tag="fps", bufs=2)
-            mc, ms = mcodes[g]
+                    ybank[b, lo] = psum.tile([P, F], F32, name="fps", tag="bank", bufs=8)
+            mc, ms = mcodes[b]
             mm(
-                ybank[b, lo][:, : hi - lo], acodes, ascales, slice(g * S, (g + 1) * S), mc, ms, slice(lo, hi),
+                ybank[b, lo][:, : hi - lo], acodes, ascales, slice(g * S, (g + 1) * S), mc, ms,
+                slice(half * F + lo, half * F + hi),
                 start=(half == 0), stop=(half == 1),
             )
 
         def y_out(b, lo, hi):
-            yo = work.tile([P, F], F32, name="yo", tag="yo", bufs=2)
+            yo = work.tile([P, F], F32, name="yo", tag="yo", bufs=3)
             nc.scalar.activation(
                 out=yo[:, : hi - lo], in_=ybank[b, lo][:, : hi - lo], func=ACT.Copy, scale=1.0 / math.sqrt(J)
             )
@@ -425,21 +453,28 @@ def tile_schnet_slot_cfconv_f5_kernel(
         log_act(0, 2, 4)
         f_mm(0)
         f_mm(1)
-        for i in range(NQ + 12):
+        logs = 2
+        exps = 0
+        weights = 0
+        ready = 0
+        quants = 0
+        mixed = 0
+        for pair in range(NQ // 2 + 4):
+            i = 2 * pair
             g, q = divmod(i, FB)
-            if q % 2 == 0 and g + 1 < NG:
-                log_act(g + 1, q, q + 2)
+            if 0 <= i - 4 < NQ:
+                back(i - 4, 2)
+            while logs < min(2 * NG, LEAD + 1 + (pair * NUM) // DEN):
+                log_act(logs // 2, logs % 2 * 2, logs % 2 * 2 + 2)
+                logs += 1
+            while exps < NG and (pair - E0) * EN // ED > exps:
+                slot_exp(exps)
+                exps += 1
             if i < NQ:
-                if i >= 4:
-                    back(i - 4)
                 min_op(i)
-            elif i < NQ + 2:
-                back(2 * i - NQ - 4)
-                back(2 * i - NQ - 3)
-            if i == 3:
-                quant_a(0)
-            if i == 7:
-                quant_a(1)
+            if quants < weights // 4:
+                quant_a(quants)
+                quants += 1
             if q == 0 and 0 <= g - 3 < NG - 1:
                 quant_m(g - 3, 0, F)
             if 0 <= i - 8 < NQ:
@@ -448,18 +483,37 @@ def tile_schnet_slot_cfconv_f5_kernel(
                 f_mm(i + 2)
             if 0 <= i - 6 < NQ:
                 h_mm(i - 6)
-            if q == 1 and 0 <= g - 3 < NG - 2:
-                y_mm(g - 3, 0, F)
-            if q == 1 and g - 3 == NG - 2:
-                y_mm(g - 3, 0, F // 2)
-                y_mm(g - 3, F // 2, F)
-            if q == 3 and 0 <= g - 3 < NG - 1 and (g - 3) % 2 == 1:
-                y_out((g - 3) // 2, 0, F)
-            if i - 8 == NQ - 2:
+            while weights + 2 <= ready:
+                slot_weights(weights, 2)
+                weights += 2
+            ready = exps
+            if i + 1 < NQ:
+                min_op(i + 1)
+            if 0 <= i - 7 < NQ:
+                mul_op(i - 7)
+            if i + 3 < NQ:
+                f_mm(i + 3)
+            if 0 <= i - 5 < NQ:
+                h_mm(i - 5)
+            if mixed < min(B - 1, 2 * quants) and 2 * mixed + 1 <= g - 3:
+                y_mm(2 * mixed, 0, F)
+                y_mm(2 * mixed + 1, 0, F)
+                y_out(mixed, 0, F)
+                mixed += 1
+            if pair == NQ // 2 + 2:
                 quant_m(NG - 1, 0, F // 2)
-                y_mm(NG - 1, 0, F // 2)
-                y_out(B - 1, 0, F // 2)
-            if i - 8 == NQ - 1:
-                quant_m(NG - 1, F // 2, F)
-                y_mm(NG - 1, F // 2, F)
-                y_out(B - 1, F // 2, F)
+        while quants < 2:
+            quant_a(quants)
+            quants += 1
+        while mixed < B - 1:
+            y_mm(2 * mixed, 0, F)
+            y_mm(2 * mixed + 1, 0, F)
+            y_out(mixed, 0, F)
+            mixed += 1
+        y_mm(NG - 2, 0, F // 2)
+        y_mm(NG - 2, F // 2, F)
+        y_mm(NG - 1, 0, F // 2)
+        y_out(B - 1, 0, F // 2)
+        quant_m(NG - 1, F // 2, F)
+        y_mm(NG - 1, F // 2, F)
+        y_out(B - 1, F // 2, F)

@@ -22,9 +22,9 @@ T = 4
 ROWS = P * T
 NG = B * J // ROWS
 FB = F // P
-VEX = []
-LEAD, NUM, DEN, E0, EN, ED = 2, 4, 3, 11, 3, 2
-AFV = (4, 5, 6, 7)
+VEX = [(1,0),(1,1)]
+LEAD, NUM, DEN, E0, EN, ED = 2, 4, 3, 10, 3, 2
+AFV = (3,6,7)
 LN2 = math.log(2.0)
 TINY = 2.0 ** -64
 
@@ -53,7 +53,7 @@ def tile_schnet_slot_cfconv_f5_kernel(
         ascales = keep.tile([P, NG * S], U8, name="ascales", align_bytes=64)
         sig = keep.tile([P, NG, FB, ROWS], F32, name="sig")
         zs = keep.tile([P, NG, T, S], F32, name="zs")
-        sc4 = keep.tile([P, T * D], F32, name="sc4")
+        sc4 = work.tile([P, T * D], F32, name="sc4", tag="sc4", bufs=1, align_bytes=64)
         ident = keep.tile([P, P], F32, name="ident")
         tiny = keep.tile([P, 1], F32, name="tiny")
         dummy = keep.tile([P, 1], F32, name="dummy")
@@ -79,12 +79,13 @@ def tile_schnet_slot_cfconv_f5_kernel(
         raw_x = {}
 
         def load_x(g):
-            xby = work.tile([P, T * D], U8, name="xby", tag="xby", bufs=4)
+            xby = work.tile([P, T * D], U8, name="xby", tag="xby", bufs=6)
             nc.sync.dma_start(out=xby[:], in_=xb_v[g])
             raw_x[g] = xby
 
         def load_r(g):
-            rld = work.tile([P, T * K], BF16, name="rld", tag="rld", bufs=2, align_bytes=64)
+            kind = ("spt", "spc")[g % 2]
+            rld = work.tile([P, T * K], BF16, name="rld" + kind, tag=kind, bufs=2, align_bytes=64)
             nc.sync.dma_start(out=rld[:], in_=rbf_v[g])
             raw_r[g] = rld
 
@@ -276,13 +277,15 @@ def tile_schnet_slot_cfconv_f5_kernel(
         def turn_r(n):
             grp_r[n] = work.tile([P, ROWS * T], BF16, name="grp", tag="grp", bufs=4, align_bytes=64)
             bank_r[n] = (turn(raw_r[n], None, n, 0), turn(raw_r[n], None, n, 1))
-            turn_out(bank_r[n][0], grp_r[n], 0, False)
+            if (n, 0) not in VEX:
+                turn_out(bank_r[n][0], grp_r[n], 0, False)
             if (n, 1) not in VEX:
                 turn_out(bank_r[n][1], grp_r[n], 1, False)
 
         def quant_r(n):
-            if (n, 1) in VEX:
-                turn_out(bank_r[n][1], grp_r[n], 1, True)
+            for b in range(2):
+                if (n, b) in VEX:
+                    turn_out(bank_r[n][b], grp_r[n], b, True)
             quant(grp_r.pop(n)[:], rcodes[:, gcols(n)], rscales[:, gcols(n)])
 
         for s in range(NG + 1):
@@ -314,7 +317,6 @@ def tile_schnet_slot_cfconv_f5_kernel(
                 )
             if s > 0:
                 quant(grp_x.pop(s - 1)[:], xcodes[:, gcols(s - 1)], xscales[:, gcols(s - 1)])
-                zbank[s - 1] = slot_mm(s - 1)
             if s > 1:
                 slot_max(s - 2)
             if s < NG:
@@ -324,6 +326,8 @@ def tile_schnet_slot_cfconv_f5_kernel(
                 turn_out(bank2, grp_x[s], 0, False)
                 if (s, 3) not in VEX:
                     turn_out(bank3, grp_x[s], 1, False)
+            if s > 0:
+                zbank[s - 1] = slot_mm(s - 1)
             if s == 0:
                 quant_r(1)
                 quant(wa_grp[:], wac[:], was[:])
@@ -379,7 +383,7 @@ def tile_schnet_slot_cfconv_f5_kernel(
         def min_op(i):
             g, q = divmod(i, FB)
             if q == 0:
-                spt[g] = work.tile([P, FB, ROWS], F32, name="spt", tag="spt", bufs=2)
+                spt[g] = work.tile([P, FB, ROWS], F32, name="spt", tag="spt", bufs=2, align_bytes=64)
             nc.vector.scalar_tensor_tensor(
                 out=spt[g][:, q, :],
                 in0=fbank.pop(i)[:],
@@ -392,7 +396,7 @@ def tile_schnet_slot_cfconv_f5_kernel(
         def back(i, n):
             g, q0 = divmod(i, FB)
             if q0 == 0:
-                spc[g] = work.tile([P, T, F], F32, name="spc", tag="spc", bufs=2)
+                spc[g] = work.tile([P, T, F], F32, name="spc", tag="spc", bufs=2, align_bytes=64)
             banks = {}
             for q in range(q0, q0 + n):
                 banks[q] = psum.tile([P, F], F32, name="tr", tag="bank", bufs=8)
@@ -410,20 +414,29 @@ def tile_schnet_slot_cfconv_f5_kernel(
             if q == 0:
                 mt[g] = work.tile([P, F * T], BF16, name="grp", tag="grp", bufs=4, align_bytes=64)
             nc.vector.tensor_tensor(
-                out=mt[g][:, q * 512 : (q + 1) * 512].rearrange("p (f t) -> p f t", t=T),
-                in0=hbank.pop(i)[:].rearrange("p t f -> p f t"),
-                in1=spc[g][:, :, q * P : (q + 1) * P].rearrange("p t f -> p f t"),
+                out=mt[g][:, q * 512 : (q + 1) * 512].rearrange("p (c i t) -> p c t i", t=T, i=4),
+                in0=hbank.pop(i)[:].rearrange("p t (c i) -> p c t i", i=4),
+                in1=spc[g][:, :, q * P : (q + 1) * P].rearrange("p t (c i) -> p c t i", i=4),
                 op=ALU.mult,
             )
 
         def quant_m(g, lo, hi):
             b, half = divmod(g, 2)
             if half == 0:
-                tag, bufs = (("rld", 2), ("rld", 2), ("xb", 3), ("wgrp", 1))[b]
-                mcodes[b] = (
-                    work.tile([P, 2 * F], U32, name="mc" + tag, tag=tag, bufs=bufs, align_bytes=64),
-                    work.tile([P, 2 * F], U8, name="ms", tag="ms", bufs=4, align_bytes=64),
-                )
+                if b == 0:
+                    pair = work.tile([P, 4 * F], U32, name="mc01", tag="sc4", bufs=1, align_bytes=64)
+                    views = pair[:, 0 : 2 * F]
+                    mcodes[1] = pair[:, 2 * F : 4 * F]
+                elif b == 1:
+                    views = mcodes[1]
+                elif b == 2:
+                    mc2 = work.tile([P, 2 * F], U32, name="mc2", tag="xb", bufs=3, align_bytes=64)
+                    views = mc2[:]
+                else:
+                    mc3 = work.tile([P, 2 * F], U32, name="mc3", tag="wgrp", bufs=1, align_bytes=64)
+                    views = mc3[:]
+                ms = work.tile([P, 2 * F], U8, name="ms", tag="ms", bufs=4, align_bytes=64)
+                mcodes[b] = (views, ms)
             mc, ms = mcodes[b]
             cols = slice(half * F + lo, half * F + hi)
             quant(mt[g][:, lo * T : hi * T], mc[:, cols], ms[:, cols])

@@ -22,9 +22,10 @@ T = 4
 ROWS = P * T
 NG = B * J // ROWS
 FB = F // P
-VEX = [(1,0),(1,1)]
-LEAD, NUM, DEN, E0, EN, ED = 2, 4, 3, 10, 3, 2
-AFV = (3,6,7)
+VEX = [(1, 0), (1, 1), (2, 3)]
+LEAD, NUM, DEN, E0, EN, ED = 2, 2, 3, 11, 3, 2
+AFV = (3, 7)
+VE = (0, 1, 25)
 LN2 = math.log(2.0)
 TINY = 2.0 ** -64
 
@@ -99,8 +100,16 @@ def tile_schnet_slot_cfconv_f5_kernel(
         nc.sync.dma_start(out=srow[0:FB, :], in_=x_scale.rearrange("o (c p) -> (o c) p", p=P))
         nc.scalar.dma_start(out=brow[0:FB, :], in_=b_f.rearrange("(c p) -> c p", p=P))
         nc.scalar.dma_start(out=brow[FB : FB + 1, :], in_=b_a.rearrange("(c p) -> c p", p=P))
-        load_r(0)
-        wf_raw = load_w(w_f, F)
+        first = work.tile([P, T * K], BF16, name="rldspt", tag="spt", bufs=2, align_bytes=64)
+        raw_r[0] = first
+        wf_raw = keep.tile([P, T, F], BF16, name="wf_raw")
+        wf_v = w_f.rearrange("(p j) f -> p j f", j=T)
+        for h in range(2):
+            half = slice(h * T * K // 2, (h + 1) * T * K // 2)
+            nc.sync.dma_start(out=first[:, half], in_=rbf_v[0][:, half])
+            nc.sync.dma_start(
+                out=wf_raw[:, :, h * F // 2 : (h + 1) * F // 2], in_=wf_v[:, :, h * F // 2 : (h + 1) * F // 2]
+            )
         load_x(0)
         load_r(1)
         wa_raw = load_w(w_a, S)
@@ -218,20 +227,24 @@ def tile_schnet_slot_cfconv_f5_kernel(
         rb0 = turn(raw_r[0], None, 0, 0)
         rb1 = turn(raw_r[0], None, 0, 1)
         turn_out(rb0, grp_r[0], 0, False)
-        turn_out(rb1, grp_r[0], 1, True)
-        nc.vector.tensor_scalar(
-            out=wf_grp[:].rearrange("p (f j) -> p f j", j=T),
-            in0=wf_raw[:].rearrange("p j f -> p f j"),
-            scalar1=-1.0,
-            scalar2=None,
-            op0=ALU.mult,
-        )
+        for h in range(2):
+            cols = slice(h * F // 2, (h + 1) * F // 2)
+            nc.vector.tensor_scalar(
+                out=wf_grp[:, h * F * T // 2 : (h + 1) * F * T // 2].rearrange("p (c i j) -> p c j i", i=4, j=T),
+                in0=wf_raw[:, :, cols].rearrange("p j (c i) -> p c j i", i=4),
+                scalar1=-1.0,
+                scalar2=None,
+                op0=ALU.mult,
+            )
+            if h == 0:
+                turn_out(rb1, grp_r[0], 1, True)
         scbank = psum.tile([P, FB, P], F32, name="hps", tag="bank", bufs=8)
         for c in range(FB):
             nc.tensor.transpose(scbank[:, c, :], sccol[:, c : c + 1].to_broadcast([P, P]), ident[:])
         nc.scalar.copy(out=sc4[:, 0:D], in_=scbank[:].rearrange("p c q -> p (c q)"))
         quant(grp_r[0][:], rcodes[:, gcols(0)], rscales[:, gcols(0)])
-        quant(wf_grp[:], wfc[:], wfs[:])
+        quant(wf_grp[:, : F * T // 2], wfc[:, : F // 2], wfs[:, : F // 2])
+        quant(wf_grp[:, F * T // 2 :], wfc[:, F // 2 :], wfs[:, F // 2 :])
         rowbank2 = psum.tile([P, P], F32, name="hps", tag="bank", bufs=8)
         nc.tensor.transpose(rowbank2[:], brow32[:], ident[:])
         nc.scalar.copy(out=nbf[:], in_=rowbank2[:, : FB + 1])
@@ -266,9 +279,9 @@ def tile_schnet_slot_cfconv_f5_kernel(
                 if g % 4 == 0:
                     at[g // 4] = work.tile([P, 4, S, T], BF16, name="at", tag="xb", bufs=3, align_bytes=64)
                 (nc.vector if g in AFV else nc.gpsimd).tensor_tensor(
-                    out=at[g // 4][:, g % 4, :, :],
-                    in0=zs[:, g, :, :].rearrange("p t n -> p n t"),
-                    in1=fac[:, g, :].unsqueeze(1).to_broadcast([P, S, T]),
+                    out=at[g // 4][:, g % 4, :, :].rearrange("p (c i) t -> p c t i", i=4),
+                    in0=zs[:, g, :, :].rearrange("p t (c i) -> p c t i", i=4),
+                    in1=fac[:, g, :].unsqueeze(1).unsqueeze(3).to_broadcast([P, S // 4, T, 4]),
                     op=ALU.mult,
                 )
 
@@ -309,8 +322,8 @@ def tile_schnet_slot_cfconv_f5_kernel(
                 turn_r(1)
                 wa_grp = work.tile([P, S * T], BF16, name="wagrp", tag="wagrp", bufs=1, align_bytes=64)
                 nc.vector.tensor_scalar(
-                    out=wa_grp[:].rearrange("p (f j) -> p f j", j=T),
-                    in0=wa_raw[:].rearrange("p j f -> p f j"),
+                    out=wa_grp[:].rearrange("p (c i j) -> p c j i", i=4, j=T),
+                    in0=wa_raw[:].rearrange("p j (c i) -> p c j i", i=4),
                     scalar1=-1.0,
                     scalar2=None,
                     op0=ALU.mult,
@@ -342,12 +355,13 @@ def tile_schnet_slot_cfconv_f5_kernel(
                 turn_out(bank3, grp_x[s], 1, True)
             if s + 2 < NG:
                 quant_r(s + 2)
-            if s == 7:
+            if s == 5:
                 wh[1] = work.tile([P, F * T], BF16, name="wgrp", tag="wgrp", bufs=1, align_bytes=64)
                 nc.vector.tensor_copy(
-                    out=wh[1][:].rearrange("p (f j) -> p f j", j=T), in_=wh[0][:].rearrange("p j f -> p f j")
+                    out=wh[1][:].rearrange("p (c i j) -> p c j i", i=4, j=T),
+                    in_=wh[0][:].rearrange("p j (c i) -> p c j i", i=4),
                 )
-            if s == 8:
+            if s == 6:
                 quant(wh[1][:], whc[:], whs[:])
         slot_max(NG - 1)
 
@@ -393,6 +407,8 @@ def tile_schnet_slot_cfconv_f5_kernel(
                 op1=ALU.min,
             )
 
+        late = {}
+
         def back(i, n):
             g, q0 = divmod(i, FB)
             if q0 == 0:
@@ -405,9 +421,18 @@ def tile_schnet_slot_cfconv_f5_kernel(
                         banks[q][:, fb * P : (fb + 1) * P], spt[g][:, fb, q * P : (q + 1) * P], ident[:]
                     )
             for q in range(q0, q0 + n):
-                nc.scalar.activation(
-                    out=spc[g][:, q, :], in_=banks[q][:], func=ACT.Copy, scale=ncut[:, g, q : q + 1]
-                )
+                if FB * g + q in VE:
+                    late[FB * g + q] = banks[q]
+                else:
+                    nc.scalar.activation(
+                        out=spc[g][:, q, :], in_=banks[q][:], func=ACT.Copy, scale=ncut[:, g, q : q + 1]
+                    )
+
+        def back_late(i):
+            g, q = divmod(i, FB)
+            nc.vector.tensor_scalar(
+                out=spc[g][:, q, :], in0=late.pop(i)[:], scalar1=ncut[:, g, q : q + 1], scalar2=None, op0=ALU.mult
+            )
 
         def mul_op(i):
             g, q = divmod(i, FB)
@@ -444,10 +469,7 @@ def tile_schnet_slot_cfconv_f5_kernel(
         def y_mm(g, lo, hi):
             b, half = divmod(g, 2)
             if half == 0:
-                if lo == 0:
-                    ybank[b, lo] = psum.tile([P, F], F32, name="hps", tag="bank", bufs=8)
-                else:
-                    ybank[b, lo] = psum.tile([P, F], F32, name="fps", tag="bank", bufs=8)
+                ybank[b, lo] = psum.tile([P, F], F32, name="yps", tag="bank", bufs=8)
             mc, ms = mcodes[b]
             mm(
                 ybank[b, lo][:, : hi - lo], acodes, ascales, slice(g * S, (g + 1) * S), mc, ms,
@@ -466,7 +488,7 @@ def tile_schnet_slot_cfconv_f5_kernel(
         log_act(0, 2, 4)
         f_mm(0)
         f_mm(1)
-        logs = 2
+        logs = 1
         exps = 0
         weights = 0
         ready = 0
@@ -477,8 +499,8 @@ def tile_schnet_slot_cfconv_f5_kernel(
             g, q = divmod(i, FB)
             if 0 <= i - 4 < NQ:
                 back(i - 4, 2)
-            while logs < min(2 * NG, LEAD + 1 + (pair * NUM) // DEN):
-                log_act(logs // 2, logs % 2 * 2, logs % 2 * 2 + 2)
+            while logs < min(NG, LEAD + (pair * NUM) // DEN):
+                log_act(logs, 0, FB)
                 logs += 1
             while exps < NG and (pair - E0) * EN // ED > exps:
                 slot_exp(exps)
@@ -502,6 +524,8 @@ def tile_schnet_slot_cfconv_f5_kernel(
             ready = exps
             if i + 1 < NQ:
                 min_op(i + 1)
+            for j in sorted(late):
+                back_late(j)
             if 0 <= i - 7 < NQ:
                 mul_op(i - 7)
             if i + 3 < NQ:
@@ -523,10 +547,18 @@ def tile_schnet_slot_cfconv_f5_kernel(
             y_mm(2 * mixed + 1, 0, F)
             y_out(mixed, 0, F)
             mixed += 1
-        y_mm(NG - 2, 0, F // 2)
-        y_mm(NG - 2, F // 2, F)
-        y_mm(NG - 1, 0, F // 2)
-        y_out(B - 1, 0, F // 2)
+        def last_mix(lo, hi):
+            bank = psum.tile([P, F], F32, name="yps", tag="bank", bufs=8)
+            mc, ms = mcodes[B - 1]
+            for half in range(2):
+                mm(
+                    bank[:, : hi - lo], acodes, ascales, slice((NG - 2 + half) * S, (NG - 1 + half) * S), mc, ms,
+                    slice(half * F + lo, half * F + hi), start=(half == 0), stop=(half == 1),
+                )
+            yo = work.tile([P, F], F32, name="yo", tag="yo", bufs=3)
+            nc.scalar.activation(out=yo[:, : hi - lo], in_=bank[:, : hi - lo], func=ACT.Copy, scale=1.0 / math.sqrt(J))
+            nc.sync.dma_start(out=out[B - 1][:, lo:hi], in_=yo[:, : hi - lo])
+
+        last_mix(0, F // 2)
         quant_m(NG - 1, F // 2, F)
-        y_mm(NG - 1, F // 2, F)
-        y_out(B - 1, F // 2, F)
+        last_mix(F // 2, F)

@@ -18,16 +18,28 @@ ACT = mybir.ActivationFunctionType
 AX = mybir.AxisListType
 
 P = 128
-T = 4
-ROWS = P * T
-NG = B * J // ROWS
-FB = F // P
-VEX = [(1, 0), (1, 1), (2, 3)]
-LEAD, NUM, DEN, E0, EN, ED = 2, 2, 3, 11, 3, 2
-AFV = (3, 7)
-VE = (0, 1, 25)
+QUAD = 4
+GROUP = P * QUAD
+GROUPS = B * J // GROUP
+BLOCKS = F // P
+ITEMS = GROUPS * BLOCKS
+BANK = 512
+BANKS = 8
+RUN = 4
+
 LN2 = math.log(2.0)
-TINY = 2.0 ** -64
+FLOOR = 2.0**-64
+
+VECTOR_RBF_COPIES = ((1, 0), (1, 1))
+VECTOR_X_COPIES = (2,)
+VECTOR_CUT_COPIES = (0, 1, 6, 19, 29)
+VECTOR_WEIGHTS = (3, 7)
+W_H_STEP = 6
+
+LN_LEAD = 2
+LN_RATE = (2, 3)
+EXP_START = 10
+EXP_RATE = (3, 2)
 
 
 def tile_schnet_slot_cfconv_f5_kernel(
@@ -40,525 +52,503 @@ def tile_schnet_slot_cfconv_f5_kernel(
         psum = ctx.enter_context(tc.psum_pool(name="psum", bufs=1))
         ctx.enter_context(tc.manual_schedule())
 
-        rcodes = keep.tile([P, NG * ROWS], U32, name="rcodes", align_bytes=64)
-        rscales = keep.tile([P, NG * ROWS], U8, name="rscales", align_bytes=64)
-        xcodes = keep.tile([P, NG * ROWS], U32, name="xcodes", align_bytes=64)
-        xscales = keep.tile([P, NG * ROWS], U8, name="xscales", align_bytes=64)
-        wfc = keep.tile([P, F], U32, name="wfc", align_bytes=64)
-        wfs = keep.tile([P, F], U8, name="wfs", align_bytes=64)
-        whc = keep.tile([P, F], U32, name="whc", align_bytes=64)
-        whs = keep.tile([P, F], U8, name="whs", align_bytes=64)
-        wac = keep.tile([P, S], U32, name="wac", align_bytes=64)
-        was = keep.tile([P, S], U8, name="was", align_bytes=64)
-        acodes = keep.tile([P, NG * S], U32, name="acodes", align_bytes=64)
-        ascales = keep.tile([P, NG * S], U8, name="ascales", align_bytes=64)
-        sig = keep.tile([P, NG, FB, ROWS], F32, name="sig")
-        zs = keep.tile([P, NG, T, S], F32, name="zs")
-        sc4 = work.tile([P, T * D], F32, name="sc4", tag="sc4", bufs=1, align_bytes=64)
+        def mx_pair(name, cols):
+            codes = keep.tile([P, cols], U32, name=name + "_codes", align_bytes=64)
+            scale_bytes = keep.tile([P, cols], U8, name=name + "_bytes", align_bytes=64)
+            return codes, scale_bytes
+
+        rbf_mx = mx_pair("rbf", GROUPS * GROUP)
+        x_mx = mx_pair("x", GROUPS * GROUP)
+        w_f_mx = mx_pair("w_f", F)
+        w_h_mx = mx_pair("w_h", F)
+        w_a_mx = mx_pair("w_a", S)
+        a_mx = mx_pair("a", GROUPS * S)
+        soft = keep.tile([P, GROUPS, BLOCKS, GROUP], F32, name="soft")
+        z = keep.tile([P, GROUPS, QUAD, S], F32, name="z")
         ident = keep.tile([P, P], F32, name="ident")
-        tiny = keep.tile([P, 1], F32, name="tiny")
-        dummy = keep.tile([P, 1], F32, name="dummy")
-        srow = keep.tile([P, P], F32, name="srow")
-        brow = keep.tile([P, P], BF16, name="brow")
-        brow32 = keep.tile([P, P], F32, name="brow32")
-        sccol = keep.tile([P, FB], F32, name="sccol")
-        nbf = keep.tile([P, FB + 1], F32, name="nbf")
-        cbf = keep.tile([P, FB], F32, name="cbf")
-        nba = keep.tile([P, S], F32, name="nba")
-        cut_raw = keep.tile([P, NG, T], BF16, name="cut_raw")
-        occ_raw = keep.tile([P, NG, T], BF16, name="occ_raw")
-        ncut = keep.tile([P, NG, T], F32, name="ncut")
-        nmax = keep.tile([P, NG, T], F32, name="nmax")
-        zsum = keep.tile([P, NG, T], F32, name="zsum")
-        rsum = keep.tile([P, NG, T], F32, name="rsum")
-        fac = keep.tile([P, NG, T], F32, name="fac")
+        floor = keep.tile([P, 1], F32, name="floor")
+        warm = keep.tile([P, 1], F32, name="warm")
+        scale_rows = keep.tile([P, P], F32, name="scale_rows")
+        bias_rows = keep.tile([P, P], BF16, name="bias_rows")
+        neg_bias_rows = keep.tile([P, P], F32, name="neg_bias_rows")
+        scale_cols = keep.tile([P, BLOCKS], F32, name="scale_cols")
+        neg_bias = keep.tile([P, BLOCKS + 1], F32, name="neg_bias")
+        ln2_bias = keep.tile([P, BLOCKS], F32, name="ln2_bias")
+        neg_b_a = keep.tile([P, S], F32, name="neg_b_a")
+        cut_raw = keep.tile([P, GROUPS, QUAD], BF16, name="cut_raw")
+        occ_raw = keep.tile([P, GROUPS, QUAD], BF16, name="occ_raw")
+        neg_cut = keep.tile([P, GROUPS, QUAD], F32, name="neg_cut")
+        neg_max = keep.tile([P, GROUPS, QUAD], F32, name="neg_max")
+        exp_sum = keep.tile([P, GROUPS, QUAD], F32, name="exp_sum")
+        inverse = keep.tile([P, GROUPS, QUAD], F32, name="inverse")
+        factor = keep.tile([P, GROUPS, QUAD], F32, name="factor")
+        scale_tile = work.tile([P, QUAD * D], F32, name="scale_tile", tag="scale_tile", bufs=1, align_bytes=64)
+        w_f_raw = keep.tile([P, QUAD, F], BF16, name="w_f_raw")
 
-        rbf_v = rbf.rearrange("(g m t) k -> g m (t k)", m=P, t=T)
-        xb_v = x_bytes.rearrange("(g m t) k -> g m (t k)", m=P, t=T)
+        def new_bank(shape, name):
+            return psum.tile(shape, F32, name=name, tag="bank", bufs=BANKS)
 
-        raw_r = {}
-        raw_x = {}
+        def new_grouped():
+            return work.tile([P, GROUP * QUAD], BF16, name="grouped", tag="grouped", bufs=4, align_bytes=64)
+
+        rbf_rows = rbf.rearrange("(g p t) k -> g p (t k)", p=P, t=QUAD)
+        x_rows = x_bytes.rearrange("(g p t) d -> g p (t d)", p=P, t=QUAD)
+        rbf_raw = {}
+        x_raw = {}
+
+        def new_rbf_raw(g):
+            tag = ("spread", "turned")[g % 2]
+            rbf_raw[g] = work.tile([P, QUAD * K], BF16, name="rbf_raw_" + tag, tag=tag, bufs=2, align_bytes=64)
+            return rbf_raw[g]
+
+        def load_rbf(g):
+            nc.sync.dma_start(out=new_rbf_raw(g)[:], in_=rbf_rows[g])
 
         def load_x(g):
-            xby = work.tile([P, T * D], U8, name="xby", tag="xby", bufs=6)
-            nc.sync.dma_start(out=xby[:], in_=xb_v[g])
-            raw_x[g] = xby
+            x_raw[g] = work.tile([P, QUAD * D], U8, name="x_raw", tag="x_raw", bufs=6)
+            nc.sync.dma_start(out=x_raw[g][:], in_=x_rows[g])
 
-        def load_r(g):
-            kind = ("spt", "spc")[g % 2]
-            rld = work.tile([P, T * K], BF16, name="rld" + kind, tag=kind, bufs=2, align_bytes=64)
-            nc.sync.dma_start(out=rld[:], in_=rbf_v[g])
-            raw_r[g] = rld
+        def load_weight(w, cols):
+            raw = work.tile([P, QUAD, cols], BF16, name="w_raw_%d" % cols, tag="w_raw_%d" % cols, bufs=1)
+            nc.sync.dma_start(out=raw[:], in_=w.rearrange("(p t) f -> p t f", t=QUAD))
+            return raw
 
-        def load_w(w, cols):
-            wld = work.tile([P, T, cols], BF16, name="wld%d" % cols, tag="wld%d" % cols, bufs=1)
-            nc.sync.dma_start(out=wld[:], in_=w.rearrange("(p j) f -> p j f", j=T))
-            return wld
+        def load_row_factor(tile, v):
+            rows = v.rearrange("b j -> (b j)").rearrange("(g p t) -> p g t", p=P, t=QUAD)
+            nc.sync.dma_start(out=tile[:], in_=rows)
 
-        nc.gpsimd.memset(srow[:], 0.0)
-        nc.gpsimd.memset(brow[:], 0.0)
-        nc.sync.dma_start(out=srow[0:FB, :], in_=x_scale.rearrange("o (c p) -> (o c) p", p=P))
-        nc.scalar.dma_start(out=brow[0:FB, :], in_=b_f.rearrange("(c p) -> c p", p=P))
-        nc.scalar.dma_start(out=brow[FB : FB + 1, :], in_=b_a.rearrange("(c p) -> c p", p=P))
-        first = work.tile([P, T * K], BF16, name="rldspt", tag="spt", bufs=2, align_bytes=64)
-        raw_r[0] = first
-        wf_raw = keep.tile([P, T, F], BF16, name="wf_raw")
-        wf_v = w_f.rearrange("(p j) f -> p j f", j=T)
-        for h in range(2):
-            half = slice(h * T * K // 2, (h + 1) * T * K // 2)
-            nc.sync.dma_start(out=first[:, half], in_=rbf_v[0][:, half])
-            nc.sync.dma_start(
-                out=wf_raw[:, :, h * F // 2 : (h + 1) * F // 2], in_=wf_v[:, :, h * F // 2 : (h + 1) * F // 2]
-            )
+        nc.gpsimd.memset(scale_rows[:], 0.0)
+        nc.gpsimd.memset(bias_rows[:], 0.0)
+        nc.sync.dma_start(out=scale_rows[0:BLOCKS, :], in_=x_scale.rearrange("o (c p) -> (o c) p", p=P))
+        nc.scalar.dma_start(out=bias_rows[0:BLOCKS, :], in_=b_f.rearrange("(c p) -> c p", p=P))
+        nc.scalar.dma_start(out=bias_rows[BLOCKS : BLOCKS + 1, :], in_=b_a.rearrange("(c p) -> c p", p=P))
+        w_f_rows = w_f.rearrange("(p t) f -> p t f", t=QUAD)
+        new_rbf_raw(0)
+        for half in range(2):
+            rows = slice(half * QUAD * K // 2, (half + 1) * QUAD * K // 2)
+            cols = slice(half * F // 2, (half + 1) * F // 2)
+            nc.sync.dma_start(out=rbf_raw[0][:, rows], in_=rbf_rows[0][:, rows])
+            nc.sync.dma_start(out=w_f_raw[:, :, cols], in_=w_f_rows[:, :, cols])
         load_x(0)
-        load_r(1)
-        wa_raw = load_w(w_a, S)
+        load_rbf(1)
+        w_a_raw = load_weight(w_a, S)
         load_x(1)
         load_x(2)
-        load_r(2)
+        load_rbf(2)
 
-        nc.gpsimd.memset(tiny[:], TINY)
+        nc.gpsimd.memset(floor[:], FLOOR)
         make_identity(nc, ident[:])
-        nc.scalar.activation(out=dummy[:], in_=tiny[:], func=ACT.Sigmoid, bias=tiny[:], scale=1.0)
+        nc.scalar.activation(out=warm[:], in_=floor[:], func=ACT.Sigmoid, bias=floor[:], scale=1.0)
 
-        grp_r = {}
-        grp_x = {}
-        xbf = {}
+        def quantize(grouped, operand, cols):
+            nc.vector.quantize_mx(out=operand[0][:, cols].bitcast(FP8X4), scales=operand[1][:, cols], in_=grouped)
 
-        def scale_x(g):
-            xb = work.tile([P, T * D], BF16, name="xb", tag="xb", bufs=3, align_bytes=64)
-            src = raw_x.pop(g)
-            if g == 0:
-                for t in range(T):
-                    cols = slice(t * D, (t + 1) * D)
-                    nc.vector.tensor_tensor(
-                        out=xb[:, cols], in0=src[:, cols].bitcast(FP8), in1=sc4[:, 0:D], op=ALU.mult
-                    )
-            else:
-                nc.vector.tensor_tensor(out=xb[:], in0=src[:].bitcast(FP8), in1=sc4[:], op=ALU.mult)
-            xbf[g] = xb
-
-        def turn(src, grp_map, g, b):
-            words = src[:].bitcast(F32)
-            bank = psum.tile([P, 2, 2, P], F32, name="tr", tag="bank", bufs=8)
-            for tt in range(2):
-                base = (2 * b + tt) * (K // 2)
-                for u in range(2):
-                    nc.tensor.transpose(bank[:, tt, u, :], words[:, base + u : base + K // 2 : 2], ident[:])
-            return bank
-
-        def turn_out(bank, grp, b, on_vector):
-            dst = grp[:].bitcast(F32)[:, b * 512 : (b + 1) * 512].rearrange("p (t r u) -> p t r u", t=2, u=2)
-            src = bank[:].rearrange("p t u r -> p t r u")
-            if on_vector:
-                nc.vector.tensor_copy(out=dst, in_=src)
-            else:
-                nc.scalar.copy(out=dst, in_=src)
-
-        pend = {}
-
-        def turn_all(src, grp_map, g, late=False):
-            grp = work.tile([P, ROWS * T], BF16, name="grp", tag="grp", bufs=4, align_bytes=64)
-            for b in range(2):
-                bank = turn(src, grp_map, g, b)
-                if late and b == 1:
-                    pend[g] = (bank, grp)
-                else:
-                    turn_out(bank, grp, b, False)
-            grp_map[g] = grp
-
-        def turn_late(g):
-            bank, grp = pend.pop(g)
-            turn_out(bank, grp, 1, True)
-
-        def quant(grp, codes, scales):
-            nc.vector.quantize_mx(out=codes.bitcast(FP8X4), scales=scales, in_=grp)
-
-        def mm(o, lc, ls, lcols, rc, rs, rcols, start=True, stop=True):
+        def mx_matmul(acc, left, left_cols, right, right_cols, start=True, stop=True):
             nc.tensor.matmul_mx(
-                out=o,
-                lhsT=lc[:, lcols].bitcast(FP8X4),
-                lhsT_scale=ls[:, lcols],
-                rhs=rc[:, rcols].bitcast(FP8X4),
-                rhs_scale=rs[:, rcols],
+                out=acc,
+                lhsT=left[0][:, left_cols].bitcast(FP8X4),
+                lhsT_scale=left[1][:, left_cols],
+                rhs=right[0][:, right_cols].bitcast(FP8X4),
+                rhs_scale=right[1][:, right_cols],
                 start=start,
                 stop=stop,
             )
 
-        def gcols(g):
-            return slice(g * ROWS, (g + 1) * ROWS)
+        def group_cols(g):
+            return slice(g * GROUP, (g + 1) * GROUP)
 
-        def filt_mm(g, fb):
-            bank = psum.tile([P, ROWS], F32, name="fps", tag="bank", bufs=8)
-            mm(bank[:], wfc, wfs, slice(fb * P, (fb + 1) * P), rcodes, rscales, gcols(g))
+        def block_cols(c):
+            return slice(c * P, (c + 1) * P)
+
+        def quad_cols(g, t):
+            return slice(g * GROUP + t * P, g * GROUP + (t + 1) * P)
+
+        def by_rows(ap):
+            return ap.rearrange("p t (c i) -> p c t i", i=RUN)
+
+        def by_columns(ap):
+            return ap.rearrange("p (c i t) -> p c t i", i=RUN, t=QUAD)
+
+        def turn(rows, b):
+            words = rows[:].bitcast(F32)
+            bank = new_bank([P, 2, 2, P], "turn_bank")
+            for t in range(2):
+                first = (2 * b + t) * (K // 2)
+                for u in range(2):
+                    nc.tensor.transpose(bank[:, t, u, :], words[:, first + u : first + K // 2 : 2], ident[:])
             return bank
 
-        def sig_act(g, fb, bank):
-            nc.scalar.activation(
-                out=sig[:, g, fb, :], in_=bank[:], func=ACT.Sigmoid, bias=nbf[:, fb : fb + 1], scale=1.0
+        def copy_turned(bank, grouped, b, copy):
+            words = grouped[:].bitcast(F32)[:, b * BANK : (b + 1) * BANK]
+            copy(
+                out=words.rearrange("p (t r u) -> p t r u", t=2, u=2), in_=bank[:].rearrange("p t u r -> p t r u")
             )
 
-        def slot_mm(g):
-            bank = psum.tile([P, T, S], F32, name="hps", tag="bank", bufs=8)
-            for t in range(T):
-                c0 = g * ROWS + t * P
-                mm(bank[:, t, :], xcodes, xscales, slice(c0, c0 + P), wac, was, slice(0, S))
+        def interleave_weight(copy_args, grouped, raw):
+            nc.vector.tensor_scalar(
+                out=by_columns(grouped), in0=by_rows(raw), scalar1=copy_args, scalar2=None, op0=ALU.mult
+            )
+
+        x_scaled = {}
+
+        def scale_x(g):
+            x_scaled[g] = work.tile([P, QUAD * D], BF16, name="x_scaled", tag="x_scaled", bufs=3, align_bytes=64)
+            for part in range(QUAD if g == 0 else 1):
+                cols = slice(part * D, (part + 1) * D) if g == 0 else slice(0, QUAD * D)
+                scales = scale_tile[:, 0:D] if g == 0 else scale_tile[:]
+                nc.vector.tensor_tensor(
+                    out=x_scaled[g][:, cols], in0=x_raw[g][:, cols].bitcast(FP8), in1=scales, op=ALU.mult
+                )
+
+        def filter_product(g, c):
+            bank = new_bank([P, GROUP], "filter_bank")
+            mx_matmul(bank[:], w_f_mx, block_cols(c), rbf_mx, group_cols(g))
             return bank
 
-        zbank = {}
+        def sigmoid(g, c, bank):
+            nc.scalar.activation(
+                out=soft[:, g, c, :], in_=bank[:], func=ACT.Sigmoid, bias=neg_bias[:, c : c + 1], scale=1.0
+            )
+
+        z_bank = {}
+
+        def slot_product(g):
+            z_bank[g] = new_bank([P, QUAD, S], "slot_bank")
+            for t in range(QUAD):
+                mx_matmul(z_bank[g][:, t, :], x_mx, quad_cols(g, t), w_a_mx, slice(0, S))
 
         def slot_bias(g):
             nc.vector.tensor_tensor(
-                out=zs[:, g, :, :],
-                in0=zbank.pop(g)[:],
-                in1=nba[:].unsqueeze(1).to_broadcast([P, T, S]),
+                out=z[:, g, :, :],
+                in0=z_bank.pop(g)[:],
+                in1=neg_b_a[:].unsqueeze(1).to_broadcast([P, QUAD, S]),
                 op=ALU.add,
             )
 
         def slot_max(g):
-            nc.vector.tensor_reduce(out=nmax[:, g, :], in_=zs[:, g, :, :], axis=AX.X, op=ALU.min)
+            nc.vector.tensor_reduce(out=neg_max[:, g, :], in_=z[:, g, :, :], axis=AX.X, op=ALU.min)
 
-        nc.gpsimd.tensor_scalar(out=brow32[:], in0=brow[:], scalar1=-1.0, scalar2=None, op0=ALU.mult)
-        wf_grp = work.tile([P, F * T], BF16, name="wgrp", tag="wgrp", bufs=1, align_bytes=64)
-        rowbank = psum.tile([P, P], F32, name="hps", tag="bank", bufs=8)
-        nc.tensor.transpose(rowbank[:], srow[:], ident[:])
-        nc.scalar.copy(out=sccol[:], in_=rowbank[:, :FB])
-        grp_r[0] = work.tile([P, ROWS * T], BF16, name="grp", tag="grp", bufs=4, align_bytes=64)
-        rb0 = turn(raw_r[0], None, 0, 0)
-        rb1 = turn(raw_r[0], None, 0, 1)
-        turn_out(rb0, grp_r[0], 0, False)
-        for h in range(2):
-            cols = slice(h * F // 2, (h + 1) * F // 2)
-            nc.vector.tensor_scalar(
-                out=wf_grp[:, h * F * T // 2 : (h + 1) * F * T // 2].rearrange("p (c i j) -> p c j i", i=4, j=T),
-                in0=wf_raw[:, :, cols].rearrange("p j (c i) -> p c j i", i=4),
-                scalar1=-1.0,
-                scalar2=None,
-                op0=ALU.mult,
-            )
-            if h == 0:
-                turn_out(rb1, grp_r[0], 1, True)
-        scbank = psum.tile([P, FB, P], F32, name="hps", tag="bank", bufs=8)
-        for c in range(FB):
-            nc.tensor.transpose(scbank[:, c, :], sccol[:, c : c + 1].to_broadcast([P, P]), ident[:])
-        nc.scalar.copy(out=sc4[:, 0:D], in_=scbank[:].rearrange("p c q -> p (c q)"))
-        quant(grp_r[0][:], rcodes[:, gcols(0)], rscales[:, gcols(0)])
-        quant(wf_grp[:, : F * T // 2], wfc[:, : F // 2], wfs[:, : F // 2])
-        quant(wf_grp[:, F * T // 2 :], wfc[:, F // 2 :], wfs[:, F // 2 :])
-        rowbank2 = psum.tile([P, P], F32, name="hps", tag="bank", bufs=8)
-        nc.tensor.transpose(rowbank2[:], brow32[:], ident[:])
-        nc.scalar.copy(out=nbf[:], in_=rowbank2[:, : FB + 1])
-        nc.gpsimd.tensor_scalar(out=cbf[:], in0=nbf[:, :FB], scalar1=LN2, scalar2=None, op0=ALU.add)
-        scale_x(0)
-        for t in range(1, T):
-            nc.scalar.copy(out=sc4[:, t * D : (t + 1) * D], in_=scbank[:].rearrange("p c q -> p (c q)"))
-        babank = psum.tile([P, S], F32, name="hps", tag="bank", bufs=8)
-        nc.tensor.transpose(babank[:], nbf[:, FB : FB + 1].to_broadcast([P, P]), ident[:])
+        rbf_grouped = {}
+        rbf_banks = {}
+        x_grouped = {}
 
-        at = {}
-        wh = {}
-
-        def slot_exp(g):
-            for t in range(T):
-                nc.scalar.activation(
-                    out=zs[:, g, t, :],
-                    in_=zs[:, g, t, :],
-                    func=ACT.Exp,
-                    bias=nmax[:, g, t : t + 1],
-                    scale=-1.0,
-                    accum_out=zsum[:, g, t : t + 1],
-                )
-
-        def slot_weights(g0, n):
-            gs = slice(g0, g0 + n)
-            nc.vector.reciprocal(out=rsum[:, gs, :], in_=zsum[:, gs, :])
-            nc.vector.scalar_tensor_tensor(
-                out=fac[:, gs, :], in0=rsum[:, gs, :], scalar=float(S), in1=occ_raw[:, gs, :], op0=ALU.mult, op1=ALU.mult
-            )
-            for g in range(g0, g0 + n):
-                if g % 4 == 0:
-                    at[g // 4] = work.tile([P, 4, S, T], BF16, name="at", tag="xb", bufs=3, align_bytes=64)
-                (nc.vector if g in AFV else nc.gpsimd).tensor_tensor(
-                    out=at[g // 4][:, g % 4, :, :].rearrange("p (c i) t -> p c t i", i=4),
-                    in0=zs[:, g, :, :].rearrange("p t (c i) -> p c t i", i=4),
-                    in1=fac[:, g, :].unsqueeze(1).unsqueeze(3).to_broadcast([P, S // 4, T, 4]),
-                    op=ALU.mult,
-                )
-
-        bank_r = {}
-
-        def turn_r(n):
-            grp_r[n] = work.tile([P, ROWS * T], BF16, name="grp", tag="grp", bufs=4, align_bytes=64)
-            bank_r[n] = (turn(raw_r[n], None, n, 0), turn(raw_r[n], None, n, 1))
-            if (n, 0) not in VEX:
-                turn_out(bank_r[n][0], grp_r[n], 0, False)
-            if (n, 1) not in VEX:
-                turn_out(bank_r[n][1], grp_r[n], 1, False)
-
-        def quant_r(n):
+        def turn_rbf(g):
+            rbf_grouped[g] = new_grouped()
+            rbf_banks[g] = [turn(rbf_raw[g], b) for b in range(2)]
             for b in range(2):
-                if (n, b) in VEX:
-                    turn_out(bank_r[n][b], grp_r[n], b, True)
-            quant(grp_r.pop(n)[:], rcodes[:, gcols(n)], rscales[:, gcols(n)])
+                if (g, b) not in VECTOR_RBF_COPIES:
+                    copy_turned(rbf_banks[g][b], rbf_grouped[g], b, nc.scalar.copy)
 
-        for s in range(NG + 1):
-            if s + 3 < NG:
-                load_r(s + 3)
+        def quantize_rbf(g):
+            for b in range(2):
+                if (g, b) in VECTOR_RBF_COPIES:
+                    copy_turned(rbf_banks[g][b], rbf_grouped[g], b, nc.vector.tensor_copy)
+            quantize(rbf_grouped[g][:], rbf_mx, group_cols(g))
+
+        nc.gpsimd.tensor_scalar(out=neg_bias_rows[:], in0=bias_rows[:], scalar1=-1.0, scalar2=None, op0=ALU.mult)
+        w_f_grouped = work.tile([P, F * QUAD], BF16, name="w_grouped", tag="w_grouped", bufs=1, align_bytes=64)
+        scale_bank = new_bank([P, P], "scale_bank")
+        nc.tensor.transpose(scale_bank[:], scale_rows[:], ident[:])
+        nc.scalar.copy(out=scale_cols[:], in_=scale_bank[:, :BLOCKS])
+        rbf_grouped[0] = new_grouped()
+        first_banks = [turn(rbf_raw[0], b) for b in range(2)]
+        copy_turned(first_banks[0], rbf_grouped[0], 0, nc.scalar.copy)
+        interleave_weight(-1.0, w_f_grouped[:, : F * QUAD // 2], w_f_raw[:, :, : F // 2])
+        copy_turned(first_banks[1], rbf_grouped[0], 1, nc.vector.tensor_copy)
+        interleave_weight(-1.0, w_f_grouped[:, F * QUAD // 2 :], w_f_raw[:, :, F // 2 :])
+        spread_bank = new_bank([P, BLOCKS, P], "spread_bank")
+        for c in range(BLOCKS):
+            nc.tensor.transpose(spread_bank[:, c, :], scale_cols[:, c : c + 1].to_broadcast([P, P]), ident[:])
+        spread_scales = spread_bank[:].rearrange("p c i -> p (c i)")
+        nc.scalar.copy(out=scale_tile[:, 0:D], in_=spread_scales)
+        quantize(rbf_grouped[0][:], rbf_mx, group_cols(0))
+        quantize(w_f_grouped[:, : F * QUAD // 2], w_f_mx, slice(0, F // 2))
+        quantize(w_f_grouped[:, F * QUAD // 2 :], w_f_mx, slice(F // 2, F))
+        bias_bank = new_bank([P, P], "bias_bank")
+        nc.tensor.transpose(bias_bank[:], neg_bias_rows[:], ident[:])
+        nc.scalar.copy(out=neg_bias[:], in_=bias_bank[:, : BLOCKS + 1])
+        nc.gpsimd.tensor_scalar(out=ln2_bias[:], in0=neg_bias[:, :BLOCKS], scalar1=LN2, scalar2=None, op0=ALU.add)
+        scale_x(0)
+        for t in range(1, QUAD):
+            nc.scalar.copy(out=scale_tile[:, t * D : (t + 1) * D], in_=spread_scales)
+        b_a_bank = new_bank([P, S], "b_a_bank")
+        nc.tensor.transpose(b_a_bank[:], neg_bias[:, BLOCKS : BLOCKS + 1].to_broadcast([P, P]), ident[:])
+
+        w_h_raw = {}
+        w_h_grouped = {}
+        for s in range(GROUPS + 1):
+            if s + 3 < GROUPS:
+                load_rbf(s + 3)
                 load_x(s + 3)
             if s == 2:
-                wh[0] = load_w(w_h, F)
+                w_h_raw[0] = load_weight(w_h, F)
             if s == 5:
-                nc.sync.dma_start(
-                    out=occ_raw[:], in_=occ.rearrange("b j -> (b j)").rearrange("(g m t) -> m g t", m=P, t=T)
-                )
-                nc.sync.dma_start(
-                    out=cut_raw[:], in_=cut.rearrange("b j -> (b j)").rearrange("(g m t) -> m g t", m=P, t=T)
-                )
-                nc.gpsimd.tensor_scalar(out=ncut[:], in0=cut_raw[:], scalar1=-1.0, scalar2=None, op0=ALU.mult)
-            if s < NG:
-                for fb in range(FB):
-                    sig_act(s, fb, filt_mm(s, fb))
+                load_row_factor(occ_raw, occ)
+                load_row_factor(cut_raw, cut)
+                nc.gpsimd.tensor_scalar(out=neg_cut[:], in0=cut_raw[:], scalar1=-1.0, scalar2=None, op0=ALU.mult)
+            if s < GROUPS:
+                for c in range(BLOCKS):
+                    sigmoid(s, c, filter_product(s, c))
             if s == 0:
-                turn_r(1)
-                wa_grp = work.tile([P, S * T], BF16, name="wagrp", tag="wagrp", bufs=1, align_bytes=64)
-                nc.vector.tensor_scalar(
-                    out=wa_grp[:].rearrange("p (c i j) -> p c j i", i=4, j=T),
-                    in0=wa_raw[:].rearrange("p j (c i) -> p c j i", i=4),
-                    scalar1=-1.0,
-                    scalar2=None,
-                    op0=ALU.mult,
-                )
+                turn_rbf(1)
+                w_a_grouped = work.tile([P, S * QUAD], BF16, name="w_a_grouped", tag="w_a_grouped", bufs=1, align_bytes=64)
+                interleave_weight(-1.0, w_a_grouped[:], w_a_raw[:])
             if s > 0:
-                quant(grp_x.pop(s - 1)[:], xcodes[:, gcols(s - 1)], xscales[:, gcols(s - 1)])
+                quantize(x_grouped[s - 1][:], x_mx, group_cols(s - 1))
             if s > 1:
                 slot_max(s - 2)
-            if s < NG:
-                grp_x[s] = work.tile([P, ROWS * T], BF16, name="grp", tag="grp", bufs=4, align_bytes=64)
-                bank2 = turn(xbf[s], None, s, 0)
-                bank3 = turn(xbf[s], None, s, 1)
-                turn_out(bank2, grp_x[s], 0, False)
-                if (s, 3) not in VEX:
-                    turn_out(bank3, grp_x[s], 1, False)
+            if s < GROUPS:
+                x_grouped[s] = new_grouped()
+                x_banks = [turn(x_scaled[s], b) for b in range(2)]
+                copy_turned(x_banks[0], x_grouped[s], 0, nc.scalar.copy)
+                if s not in VECTOR_X_COPIES:
+                    copy_turned(x_banks[1], x_grouped[s], 1, nc.scalar.copy)
             if s > 0:
-                zbank[s - 1] = slot_mm(s - 1)
+                slot_product(s - 1)
             if s == 0:
-                quant_r(1)
-                quant(wa_grp[:], wac[:], was[:])
-                nc.vector.tensor_copy(out=nba[:], in_=babank[:])
-            if s + 2 < NG:
-                turn_r(s + 2)
-            if s + 1 < NG:
+                quantize_rbf(1)
+                quantize(w_a_grouped[:], w_a_mx, slice(0, S))
+                nc.vector.tensor_copy(out=neg_b_a[:], in_=b_a_bank[:])
+            if s + 2 < GROUPS:
+                turn_rbf(s + 2)
+            if s + 1 < GROUPS:
                 scale_x(s + 1)
             if s > 0:
                 slot_bias(s - 1)
-            if s < NG and (s, 3) in VEX:
-                turn_out(bank3, grp_x[s], 1, True)
-            if s + 2 < NG:
-                quant_r(s + 2)
-            if s == 5:
-                wh[1] = work.tile([P, F * T], BF16, name="wgrp", tag="wgrp", bufs=1, align_bytes=64)
-                nc.vector.tensor_copy(
-                    out=wh[1][:].rearrange("p (c i j) -> p c j i", i=4, j=T),
-                    in_=wh[0][:].rearrange("p j (c i) -> p c j i", i=4),
+            if s in VECTOR_X_COPIES:
+                copy_turned(x_banks[1], x_grouped[s], 1, nc.vector.tensor_copy)
+            if s + 2 < GROUPS:
+                quantize_rbf(s + 2)
+            if s == W_H_STEP:
+                w_h_grouped[0] = work.tile(
+                    [P, F * QUAD], BF16, name="w_grouped", tag="w_grouped", bufs=1, align_bytes=64
                 )
-            if s == 6:
-                quant(wh[1][:], whc[:], whs[:])
-        slot_max(NG - 1)
+                nc.vector.tensor_copy(out=by_columns(w_h_grouped[0][:]), in_=by_rows(w_h_raw[0][:]))
+            if s == W_H_STEP + 1:
+                quantize(w_h_grouped[0][:], w_h_mx, slice(0, F))
+        slot_max(GROUPS - 1)
 
-        def quant_a(h):
-            cols = slice(h * 4 * S, (h + 1) * 4 * S)
-            quant(at[h][:].rearrange("p g n t -> p (g n t)"), acodes[:, cols], ascales[:, cols])
-
-        def log_act(g, lo, hi):
+        def logarithm(g, c0, c1):
             nc.scalar.activation(
-                out=sig[:, g, lo:hi, :], in_=sig[:, g, lo:hi, :], func=ACT.Ln, bias=tiny[:], scale=2.0
+                out=soft[:, g, c0:c1, :], in_=soft[:, g, c0:c1, :], func=ACT.Ln, bias=floor[:], scale=2.0
             )
 
-        spt = {}
-        spc = {}
-        mt = {}
-        fbank = {}
-        hbank = {}
-        ybank = {}
-        mcodes = {}
-        NQ = NG * FB
+        filter_bank = {}
+        spread = {}
 
-        def h_mm(i):
-            g, q = divmod(i, FB)
-            hbank[i] = psum.tile([P, T, P], F32, name="hps", tag="bank", bufs=8)
-            for t in range(T):
-                c0 = g * ROWS + t * P
-                mm(hbank[i][:, t, :], xcodes, xscales, slice(c0, c0 + P), whc, whs, slice(q * P, (q + 1) * P))
+        def product_again(i):
+            filter_bank[i] = filter_product(i // BLOCKS, i % BLOCKS)
 
-        def f_mm(i):
-            g, q = divmod(i, FB)
-            fbank[i] = filt_mm(g, q)
-
-        def min_op(i):
-            g, q = divmod(i, FB)
-            if q == 0:
-                spt[g] = work.tile([P, FB, ROWS], F32, name="spt", tag="spt", bufs=2, align_bytes=64)
+        def minimum(i):
+            g, c = divmod(i, BLOCKS)
+            if c == 0:
+                spread[g] = work.tile([P, BLOCKS, GROUP], F32, name="spread", tag="spread", bufs=2, align_bytes=64)
             nc.vector.scalar_tensor_tensor(
-                out=spt[g][:, q, :],
-                in0=fbank.pop(i)[:],
-                scalar=cbf[:, q : q + 1],
-                in1=sig[:, g, q, :],
+                out=spread[g][:, c, :],
+                in0=filter_bank.pop(i)[:],
+                scalar=ln2_bias[:, c : c + 1],
+                in1=soft[:, g, c, :],
                 op0=ALU.add,
                 op1=ALU.min,
             )
 
-        late = {}
+        turned = {}
+        late_banks = {}
 
-        def back(i, n):
-            g, q0 = divmod(i, FB)
-            if q0 == 0:
-                spc[g] = work.tile([P, T, F], F32, name="spc", tag="spc", bufs=2, align_bytes=64)
+        def turn_back(i):
+            g, t0 = divmod(i, QUAD)
+            if t0 == 0:
+                turned[g] = work.tile([P, QUAD, F], F32, name="turned", tag="turned", bufs=2, align_bytes=64)
             banks = {}
-            for q in range(q0, q0 + n):
-                banks[q] = psum.tile([P, F], F32, name="tr", tag="bank", bufs=8)
-                for fb in range(FB):
-                    nc.tensor.transpose(
-                        banks[q][:, fb * P : (fb + 1) * P], spt[g][:, fb, q * P : (q + 1) * P], ident[:]
-                    )
-            for q in range(q0, q0 + n):
-                if FB * g + q in VE:
-                    late[FB * g + q] = banks[q]
+            for t in range(t0, t0 + 2):
+                banks[t] = new_bank([P, F], "back_bank")
+                for c in range(BLOCKS):
+                    nc.tensor.transpose(banks[t][:, block_cols(c)], spread[g][:, c, block_cols(t)], ident[:])
+            for t in range(t0, t0 + 2):
+                if QUAD * g + t in VECTOR_CUT_COPIES:
+                    late_banks[g, t] = banks[t]
                 else:
                     nc.scalar.activation(
-                        out=spc[g][:, q, :], in_=banks[q][:], func=ACT.Copy, scale=ncut[:, g, q : q + 1]
+                        out=turned[g][:, t, :], in_=banks[t][:], func=ACT.Copy, scale=neg_cut[:, g, t : t + 1]
                     )
 
-        def back_late(i):
-            g, q = divmod(i, FB)
-            nc.vector.tensor_scalar(
-                out=spc[g][:, q, :], in0=late.pop(i)[:], scalar1=ncut[:, g, q : q + 1], scalar2=None, op0=ALU.mult
-            )
+        def late_copies():
+            for g, t in sorted(late_banks):
+                nc.vector.tensor_scalar(
+                    out=turned[g][:, t, :],
+                    in0=late_banks[g, t][:],
+                    scalar1=neg_cut[:, g, t : t + 1],
+                    scalar2=None,
+                    op0=ALU.mult,
+                )
+            late_banks.clear()
 
-        def mul_op(i):
-            g, q = divmod(i, FB)
-            if q == 0:
-                mt[g] = work.tile([P, F * T], BF16, name="grp", tag="grp", bufs=4, align_bytes=64)
+        h_bank = {}
+        m_grouped = {}
+
+        def feature_product(i):
+            g, c = divmod(i, BLOCKS)
+            h_bank[i] = new_bank([P, QUAD, P], "feature_bank")
+            for t in range(QUAD):
+                mx_matmul(h_bank[i][:, t, :], x_mx, quad_cols(g, t), w_h_mx, block_cols(c))
+
+        def message(i):
+            g, c = divmod(i, BLOCKS)
+            if c == 0:
+                m_grouped[g] = new_grouped()
             nc.vector.tensor_tensor(
-                out=mt[g][:, q * 512 : (q + 1) * 512].rearrange("p (c i t) -> p c t i", t=T, i=4),
-                in0=hbank.pop(i)[:].rearrange("p t (c i) -> p c t i", i=4),
-                in1=spc[g][:, :, q * P : (q + 1) * P].rearrange("p t (c i) -> p c t i", i=4),
+                out=by_columns(m_grouped[g][:, c * QUAD * P : (c + 1) * QUAD * P]),
+                in0=by_rows(h_bank.pop(i)[:]),
+                in1=by_rows(turned[g][:, :, block_cols(c)]),
                 op=ALU.mult,
             )
 
-        def quant_m(g, lo, hi):
+        m_codes = {}
+        m_mx = {}
+
+        def open_environment(b):
+            if b == 0:
+                codes = work.tile([P, 4 * F], U32, name="m_codes_01", tag="scale_tile", bufs=1, align_bytes=64)
+                m_codes[0] = codes[:, : 2 * F]
+                m_codes[1] = codes[:, 2 * F :]
+            if b == 2:
+                codes = work.tile([P, 2 * F], U32, name="m_codes_2", tag="x_scaled", bufs=3, align_bytes=64)
+                m_codes[2] = codes[:]
+            if b == 3:
+                codes = work.tile([P, 2 * F], U32, name="m_codes_3", tag="w_grouped", bufs=1, align_bytes=64)
+                m_codes[3] = codes[:]
+            m_bytes = work.tile([P, 2 * F], U8, name="m_bytes", tag="m_bytes", bufs=4, align_bytes=64)
+            m_mx[b] = (m_codes[b], m_bytes)
+
+        def quantize_m(g, f0, f1):
             b, half = divmod(g, 2)
             if half == 0:
-                if b == 0:
-                    pair = work.tile([P, 4 * F], U32, name="mc01", tag="sc4", bufs=1, align_bytes=64)
-                    views = pair[:, 0 : 2 * F]
-                    mcodes[1] = pair[:, 2 * F : 4 * F]
-                elif b == 1:
-                    views = mcodes[1]
-                elif b == 2:
-                    mc2 = work.tile([P, 2 * F], U32, name="mc2", tag="xb", bufs=3, align_bytes=64)
-                    views = mc2[:]
-                else:
-                    mc3 = work.tile([P, 2 * F], U32, name="mc3", tag="wgrp", bufs=1, align_bytes=64)
-                    views = mc3[:]
-                ms = work.tile([P, 2 * F], U8, name="ms", tag="ms", bufs=4, align_bytes=64)
-                mcodes[b] = (views, ms)
-            mc, ms = mcodes[b]
-            cols = slice(half * F + lo, half * F + hi)
-            quant(mt[g][:, lo * T : hi * T], mc[:, cols], ms[:, cols])
+                open_environment(b)
+            quantize(m_grouped[g][:, f0 * QUAD : f1 * QUAD], m_mx[b], slice(half * F + f0, half * F + f1))
 
-        def y_mm(g, lo, hi):
-            b, half = divmod(g, 2)
-            if half == 0:
-                ybank[b, lo] = psum.tile([P, F], F32, name="yps", tag="bank", bufs=8)
-            mc, ms = mcodes[b]
-            mm(
-                ybank[b, lo][:, : hi - lo], acodes, ascales, slice(g * S, (g + 1) * S), mc, ms,
-                slice(half * F + lo, half * F + hi),
-                start=(half == 0), stop=(half == 1),
+        def exponential(g):
+            for t in range(QUAD):
+                nc.scalar.activation(
+                    out=z[:, g, t, :],
+                    in_=z[:, g, t, :],
+                    func=ACT.Exp,
+                    bias=neg_max[:, g, t : t + 1],
+                    scale=-1.0,
+                    accum_out=exp_sum[:, g, t : t + 1],
+                )
+
+        def weight_inverse(g0):
+            nc.vector.reciprocal(out=inverse[:, g0 : g0 + 2, :], in_=exp_sum[:, g0 : g0 + 2, :])
+
+        def weight_factor(g0):
+            nc.vector.scalar_tensor_tensor(
+                out=factor[:, g0 : g0 + 2, :],
+                in0=inverse[:, g0 : g0 + 2, :],
+                scalar=float(S),
+                in1=occ_raw[:, g0 : g0 + 2, :],
+                op0=ALU.mult,
+                op1=ALU.mult,
             )
 
-        def y_out(b, lo, hi):
-            yo = work.tile([P, F], F32, name="yo", tag="yo", bufs=3)
-            nc.scalar.activation(
-                out=yo[:, : hi - lo], in_=ybank[b, lo][:, : hi - lo], func=ACT.Copy, scale=1.0 / math.sqrt(J)
-            )
-            nc.sync.dma_start(out=out[b][:, lo:hi], in_=yo[:, : hi - lo])
+        a_grouped = {}
 
-        log_act(0, 0, 2)
-        log_act(0, 2, 4)
-        f_mm(0)
-        f_mm(1)
+        def weight_product(g0):
+            for g in range(g0, g0 + 2):
+                h, part = divmod(g, GROUPS // 2)
+                if part == 0:
+                    a_grouped[h] = work.tile(
+                        [P, GROUPS // 2, S * QUAD], BF16, name="a_grouped", tag="x_scaled", bufs=3, align_bytes=64
+                    )
+                engine = nc.vector if g in VECTOR_WEIGHTS else nc.gpsimd
+                engine.tensor_tensor(
+                    out=by_columns(a_grouped[h][:, part, :]),
+                    in0=by_rows(z[:, g, :, :]),
+                    in1=factor[:, g, :].unsqueeze(1).unsqueeze(3).to_broadcast([P, S // RUN, QUAD, RUN]),
+                    op=ALU.mult,
+                )
+
+        def quantize_a(h):
+            cols = slice(h * GROUPS // 2 * S, (h + 1) * GROUPS // 2 * S)
+            quantize(a_grouped[h][:].rearrange("p g n -> p (g n)"), a_mx, cols)
+
+        def mix(b, f0, f1):
+            bank = new_bank([P, F], "mix_bank")
+            for half in range(2):
+                g = 2 * b + half
+                mx_matmul(
+                    bank[:, : f1 - f0],
+                    a_mx,
+                    slice(g * S, (g + 1) * S),
+                    m_mx[b],
+                    slice(half * F + f0, half * F + f1),
+                    start=(half == 0),
+                    stop=(half == 1),
+                )
+            name = "y_%d" % (f1 - f0)
+            y = work.tile([P, f1 - f0], F32, name=name, tag=name, bufs=2)
+            nc.scalar.activation(out=y[:], in_=bank[:, : f1 - f0], func=ACT.Copy, scale=1.0 / math.sqrt(J))
+            nc.sync.dma_start(out=out[b][:, f0:f1], in_=y[:])
+
+        def do(step, item):
+            if 0 <= item < ITEMS:
+                step(item)
+
+        logarithm(0, 0, BLOCKS // 2)
+        logarithm(0, BLOCKS // 2, BLOCKS)
+        product_again(0)
+        product_again(1)
         logs = 1
         exps = 0
-        weights = 0
-        ready = 0
-        quants = 0
+        summed = 0
+        weighted = 0
+        a_done = 0
         mixed = 0
-        for pair in range(NQ // 2 + 4):
-            i = 2 * pair
-            g, q = divmod(i, FB)
-            if 0 <= i - 4 < NQ:
-                back(i - 4, 2)
-            while logs < min(NG, LEAD + (pair * NUM) // DEN):
-                log_act(logs, 0, FB)
+        for n in range(ITEMS // 2 + 4):
+            i = 2 * n
+            g, c = divmod(i, BLOCKS)
+            do(turn_back, i - 4)
+            while logs < min(GROUPS, LN_LEAD + n * LN_RATE[0] // LN_RATE[1]):
+                logarithm(logs, 0, BLOCKS)
                 logs += 1
-            while exps < NG and (pair - E0) * EN // ED > exps:
-                slot_exp(exps)
+            while exps < min(GROUPS, (n - EXP_START) * EXP_RATE[0] // EXP_RATE[1]):
+                exponential(exps)
                 exps += 1
-            if i < NQ:
-                min_op(i)
-            if quants < weights // 4:
-                quant_a(quants)
-                quants += 1
-            if q == 0 and 0 <= g - 3 < NG - 1:
-                quant_m(g - 3, 0, F)
-            if 0 <= i - 8 < NQ:
-                mul_op(i - 8)
-            if i + 2 < NQ:
-                f_mm(i + 2)
-            if 0 <= i - 6 < NQ:
-                h_mm(i - 6)
-            while weights + 2 <= ready:
-                slot_weights(weights, 2)
-                weights += 2
-            ready = exps
-            if i + 1 < NQ:
-                min_op(i + 1)
-            for j in sorted(late):
-                back_late(j)
-            if 0 <= i - 7 < NQ:
-                mul_op(i - 7)
-            if i + 3 < NQ:
-                f_mm(i + 3)
-            if 0 <= i - 5 < NQ:
-                h_mm(i - 5)
-            if mixed < min(B - 1, 2 * quants) and 2 * mixed + 1 <= g - 3:
-                y_mm(2 * mixed, 0, F)
-                y_mm(2 * mixed + 1, 0, F)
-                y_out(mixed, 0, F)
+            weigh = weighted + 2 <= summed
+            summed = exps
+            do(minimum, i)
+            if c == 0 and 0 <= g - 3 < GROUPS - 1:
+                quantize_m(g - 3, 0, F)
+            if weigh:
+                weight_inverse(weighted)
+            do(message, i - 8)
+            do(product_again, i + 2)
+            do(feature_product, i - 6)
+            do(minimum, i + 1)
+            if a_done < weighted // 4:
+                quantize_a(a_done)
+                a_done += 1
+            if weigh:
+                weight_factor(weighted)
+            if n == ITEMS // 2 + 3:
+                quantize_m(GROUPS - 1, 0, F // 2)
+            late_copies()
+            do(message, i - 7)
+            do(product_again, i + 3)
+            do(feature_product, i - 5)
+            if weigh:
+                weight_product(weighted)
+                weighted += 2
+            if mixed < min(B - 1, 2 * a_done) and 2 * mixed + 1 <= g - 3:
+                mix(mixed, 0, F)
                 mixed += 1
-            if pair == NQ // 2 + 2:
-                quant_m(NG - 1, 0, F // 2)
-        while quants < 2:
-            quant_a(quants)
-            quants += 1
+        while a_done < 2:
+            quantize_a(a_done)
+            a_done += 1
         while mixed < B - 1:
-            y_mm(2 * mixed, 0, F)
-            y_mm(2 * mixed + 1, 0, F)
-            y_out(mixed, 0, F)
+            mix(mixed, 0, F)
             mixed += 1
-        def last_mix(lo, hi):
-            bank = psum.tile([P, F], F32, name="yps", tag="bank", bufs=8)
-            mc, ms = mcodes[B - 1]
-            for half in range(2):
-                mm(
-                    bank[:, : hi - lo], acodes, ascales, slice((NG - 2 + half) * S, (NG - 1 + half) * S), mc, ms,
-                    slice(half * F + lo, half * F + hi), start=(half == 0), stop=(half == 1),
-                )
-            yo = work.tile([P, F], F32, name="yo", tag="yo", bufs=3)
-            nc.scalar.activation(out=yo[:, : hi - lo], in_=bank[:, : hi - lo], func=ACT.Copy, scale=1.0 / math.sqrt(J))
-            nc.sync.dma_start(out=out[B - 1][:, lo:hi], in_=yo[:, : hi - lo])
-
-        last_mix(0, F // 2)
-        quant_m(NG - 1, F // 2, F)
-        last_mix(F // 2, F)
+        quantize_m(GROUPS - 1, F // 2, 3 * F // 4)
+        mix(B - 1, 0, F // 2)
+        quantize_m(GROUPS - 1, 3 * F // 4, F)
+        mix(B - 1, F // 2, 3 * F // 4)
+        mix(B - 1, 3 * F // 4, F)

import math
from contextlib import ExitStack

import concourse.mybir as mybir
from concourse.masks import make_identity

B, J, K, D, F, S = 4, 1024, 512, 512, 512, 128
FLOPS = 2 * B * J * (K * F + D * F + D * S) + 2 * B * S * J * F

F32 = mybir.dt.float32
BF16 = mybir.dt.bfloat16
U32 = mybir.dt.uint32
U8 = mybir.dt.uint8
FP8 = mybir.dt.float8_e4m3fn
FP8X4 = mybir.dt.float8_e4m3fn_x4
ALU = mybir.AluOpType
ACT = mybir.ActivationFunctionType
AX = mybir.AxisListType

P = 128
QUAD = 4
GROUP = P * QUAD
GROUPS = B * J // GROUP
BLOCKS = F // P
ITEMS = GROUPS * BLOCKS
BANK = 512
BANKS = 8
RUN = 4

LN2 = math.log(2.0)
FLOOR = 2.0**-64

VECTOR_RBF_COPIES = ((1, 0), (1, 1))
VECTOR_X_COPIES = (2,)
VECTOR_CUT_COPIES = (0, 1, 6, 19, 29)
VECTOR_WEIGHTS = (3, 7)
W_H_STEP = 6

LN_LEAD = 2
LN_RATE = (2, 3)
EXP_START = 10
EXP_RATE = (3, 2)


def tile_schnet_slot_cfconv_f5_kernel(
    tc, rbf, x_bytes, x_scale, cut, occ, w_f, b_f, w_h, w_a, b_a, out
):
    nc = tc.nc
    with ExitStack() as ctx:
        keep = ctx.enter_context(tc.tile_pool(name="keep", bufs=1))
        work = ctx.enter_context(tc.tile_pool(name="work", bufs=2))
        psum = ctx.enter_context(tc.psum_pool(name="psum", bufs=1))
        ctx.enter_context(tc.manual_schedule())

        def mx_pair(name, cols):
            codes = keep.tile([P, cols], U32, name=name + "_codes", align_bytes=64)
            scale_bytes = keep.tile([P, cols], U8, name=name + "_bytes", align_bytes=64)
            return codes, scale_bytes

        rbf_mx = mx_pair("rbf", GROUPS * GROUP)
        x_mx = mx_pair("x", GROUPS * GROUP)
        w_f_mx = mx_pair("w_f", F)
        w_h_mx = mx_pair("w_h", F)
        w_a_mx = mx_pair("w_a", S)
        a_mx = mx_pair("a", GROUPS * S)
        soft = keep.tile([P, GROUPS, BLOCKS, GROUP], F32, name="soft")
        z = keep.tile([P, GROUPS, QUAD, S], F32, name="z")
        ident = keep.tile([P, P], F32, name="ident")
        floor = keep.tile([P, 1], F32, name="floor")
        warm = keep.tile([P, 1], F32, name="warm")
        scale_rows = keep.tile([P, P], F32, name="scale_rows")
        bias_rows = keep.tile([P, P], BF16, name="bias_rows")
        neg_bias_rows = keep.tile([P, P], F32, name="neg_bias_rows")
        scale_cols = keep.tile([P, BLOCKS], F32, name="scale_cols")
        neg_bias = keep.tile([P, BLOCKS + 1], F32, name="neg_bias")
        ln2_bias = keep.tile([P, BLOCKS], F32, name="ln2_bias")
        neg_b_a = keep.tile([P, S], F32, name="neg_b_a")
        cut_raw = keep.tile([P, GROUPS, QUAD], BF16, name="cut_raw")
        occ_raw = keep.tile([P, GROUPS, QUAD], BF16, name="occ_raw")
        neg_cut = keep.tile([P, GROUPS, QUAD], F32, name="neg_cut")
        neg_max = keep.tile([P, GROUPS, QUAD], F32, name="neg_max")
        exp_sum = keep.tile([P, GROUPS, QUAD], F32, name="exp_sum")
        inverse = keep.tile([P, GROUPS, QUAD], F32, name="inverse")
        factor = keep.tile([P, GROUPS, QUAD], F32, name="factor")
        scale_tile = work.tile([P, QUAD * D], F32, name="scale_tile", tag="scale_tile", bufs=1, align_bytes=64)
        w_f_raw = keep.tile([P, QUAD, F], BF16, name="w_f_raw")

        def new_bank(shape, name):
            return psum.tile(shape, F32, name=name, tag="bank", bufs=BANKS)

        def new_grouped():
            return work.tile([P, GROUP * QUAD], BF16, name="grouped", tag="grouped", bufs=4, align_bytes=64)

        rbf_rows = rbf.rearrange("(g p t) k -> g p (t k)", p=P, t=QUAD)
        x_rows = x_bytes.rearrange("(g p t) d -> g p (t d)", p=P, t=QUAD)
        rbf_raw = {}
        x_raw = {}

        def new_rbf_raw(g):
            tag = ("spread", "turned")[g % 2]
            rbf_raw[g] = work.tile([P, QUAD * K], BF16, name="rbf_raw_" + tag, tag=tag, bufs=2, align_bytes=64)
            return rbf_raw[g]

        def load_rbf(g):
            nc.sync.dma_start(out=new_rbf_raw(g)[:], in_=rbf_rows[g])

        def load_x(g):
            x_raw[g] = work.tile([P, QUAD * D], U8, name="x_raw", tag="x_raw", bufs=6)
            nc.sync.dma_start(out=x_raw[g][:], in_=x_rows[g])

        def load_weight(w, cols):
            raw = work.tile([P, QUAD, cols], BF16, name="w_raw_%d" % cols, tag="w_raw_%d" % cols, bufs=1)
            nc.sync.dma_start(out=raw[:], in_=w.rearrange("(p t) f -> p t f", t=QUAD))
            return raw

        def load_row_factor(tile, v):
            rows = v.rearrange("b j -> (b j)").rearrange("(g p t) -> p g t", p=P, t=QUAD)
            nc.sync.dma_start(out=tile[:], in_=rows)

        nc.gpsimd.memset(scale_rows[:], 0.0)
        nc.gpsimd.memset(bias_rows[:], 0.0)
        nc.sync.dma_start(out=scale_rows[0:BLOCKS, :], in_=x_scale.rearrange("o (c p) -> (o c) p", p=P))
        nc.scalar.dma_start(out=bias_rows[0:BLOCKS, :], in_=b_f.rearrange("(c p) -> c p", p=P))
        nc.scalar.dma_start(out=bias_rows[BLOCKS : BLOCKS + 1, :], in_=b_a.rearrange("(c p) -> c p", p=P))
        w_f_rows = w_f.rearrange("(p t) f -> p t f", t=QUAD)
        new_rbf_raw(0)
        for half in range(2):
            rows = slice(half * QUAD * K // 2, (half + 1) * QUAD * K // 2)
            cols = slice(half * F // 2, (half + 1) * F // 2)
            nc.sync.dma_start(out=rbf_raw[0][:, rows], in_=rbf_rows[0][:, rows])
            nc.sync.dma_start(out=w_f_raw[:, :, cols], in_=w_f_rows[:, :, cols])
        load_x(0)
        load_rbf(1)
        w_a_raw = load_weight(w_a, S)
        load_x(1)
        load_x(2)
        load_rbf(2)

        nc.gpsimd.memset(floor[:], FLOOR)
        make_identity(nc, ident[:])
        nc.scalar.activation(out=warm[:], in_=floor[:], func=ACT.Sigmoid, bias=floor[:], scale=1.0)

        def quantize(grouped, operand, cols):
            nc.vector.quantize_mx(out=operand[0][:, cols].bitcast(FP8X4), scales=operand[1][:, cols], in_=grouped)

        def mx_matmul(acc, left, left_cols, right, right_cols, start=True, stop=True):
            nc.tensor.matmul_mx(
                out=acc,
                lhsT=left[0][:, left_cols].bitcast(FP8X4),
                lhsT_scale=left[1][:, left_cols],
                rhs=right[0][:, right_cols].bitcast(FP8X4),
                rhs_scale=right[1][:, right_cols],
                start=start,
                stop=stop,
            )

        def group_cols(g):
            return slice(g * GROUP, (g + 1) * GROUP)

        def block_cols(c):
            return slice(c * P, (c + 1) * P)

        def quad_cols(g, t):
            return slice(g * GROUP + t * P, g * GROUP + (t + 1) * P)

        def by_rows(ap):
            return ap.rearrange("p t (c i) -> p c t i", i=RUN)

        def by_columns(ap):
            return ap.rearrange("p (c i t) -> p c t i", i=RUN, t=QUAD)

        def turn(rows, b):
            words = rows[:].bitcast(F32)
            bank = new_bank([P, 2, 2, P], "turn_bank")
            for t in range(2):
                first = (2 * b + t) * (K // 2)
                for u in range(2):
                    nc.tensor.transpose(bank[:, t, u, :], words[:, first + u : first + K // 2 : 2], ident[:])
            return bank

        def copy_turned(bank, grouped, b, copy):
            words = grouped[:].bitcast(F32)[:, b * BANK : (b + 1) * BANK]
            copy(
                out=words.rearrange("p (t r u) -> p t r u", t=2, u=2), in_=bank[:].rearrange("p t u r -> p t r u")
            )

        def interleave_weight(copy_args, grouped, raw):
            nc.vector.tensor_scalar(
                out=by_columns(grouped), in0=by_rows(raw), scalar1=copy_args, scalar2=None, op0=ALU.mult
            )

        x_scaled = {}

        def scale_x(g):
            x_scaled[g] = work.tile([P, QUAD * D], BF16, name="x_scaled", tag="x_scaled", bufs=3, align_bytes=64)
            for part in range(QUAD if g == 0 else 1):
                cols = slice(part * D, (part + 1) * D) if g == 0 else slice(0, QUAD * D)
                scales = scale_tile[:, 0:D] if g == 0 else scale_tile[:]
                nc.vector.tensor_tensor(
                    out=x_scaled[g][:, cols], in0=x_raw[g][:, cols].bitcast(FP8), in1=scales, op=ALU.mult
                )

        def filter_product(g, c):
            bank = new_bank([P, GROUP], "filter_bank")
            mx_matmul(bank[:], w_f_mx, block_cols(c), rbf_mx, group_cols(g))
            return bank

        def sigmoid(g, c, bank):
            nc.scalar.activation(
                out=soft[:, g, c, :], in_=bank[:], func=ACT.Sigmoid, bias=neg_bias[:, c : c + 1], scale=1.0
            )

        z_bank = {}

        def slot_product(g):
            z_bank[g] = new_bank([P, QUAD, S], "slot_bank")
            for t in range(QUAD):
                mx_matmul(z_bank[g][:, t, :], x_mx, quad_cols(g, t), w_a_mx, slice(0, S))

        def slot_bias(g):
            nc.vector.tensor_tensor(
                out=z[:, g, :, :],
                in0=z_bank.pop(g)[:],
                in1=neg_b_a[:].unsqueeze(1).to_broadcast([P, QUAD, S]),
                op=ALU.add,
            )

        def slot_max(g):
            nc.vector.tensor_reduce(out=neg_max[:, g, :], in_=z[:, g, :, :], axis=AX.X, op=ALU.min)

        rbf_grouped = {}
        rbf_banks = {}
        x_grouped = {}

        def turn_rbf(g):
            rbf_grouped[g] = new_grouped()
            rbf_banks[g] = [turn(rbf_raw[g], b) for b in range(2)]
            for b in range(2):
                if (g, b) not in VECTOR_RBF_COPIES:
                    copy_turned(rbf_banks[g][b], rbf_grouped[g], b, nc.scalar.copy)

        def quantize_rbf(g):
            for b in range(2):
                if (g, b) in VECTOR_RBF_COPIES:
                    copy_turned(rbf_banks[g][b], rbf_grouped[g], b, nc.vector.tensor_copy)
            quantize(rbf_grouped[g][:], rbf_mx, group_cols(g))

        nc.gpsimd.tensor_scalar(out=neg_bias_rows[:], in0=bias_rows[:], scalar1=-1.0, scalar2=None, op0=ALU.mult)
        w_f_grouped = work.tile([P, F * QUAD], BF16, name="w_grouped", tag="w_grouped", bufs=1, align_bytes=64)
        scale_bank = new_bank([P, P], "scale_bank")
        nc.tensor.transpose(scale_bank[:], scale_rows[:], ident[:])
        nc.scalar.copy(out=scale_cols[:], in_=scale_bank[:, :BLOCKS])
        rbf_grouped[0] = new_grouped()
        first_banks = [turn(rbf_raw[0], b) for b in range(2)]
        copy_turned(first_banks[0], rbf_grouped[0], 0, nc.scalar.copy)
        interleave_weight(-1.0, w_f_grouped[:, : F * QUAD // 2], w_f_raw[:, :, : F // 2])
        copy_turned(first_banks[1], rbf_grouped[0], 1, nc.vector.tensor_copy)
        interleave_weight(-1.0, w_f_grouped[:, F * QUAD // 2 :], w_f_raw[:, :, F // 2 :])
        spread_bank = new_bank([P, BLOCKS, P], "spread_bank")
        for c in range(BLOCKS):
            nc.tensor.transpose(spread_bank[:, c, :], scale_cols[:, c : c + 1].to_broadcast([P, P]), ident[:])
        spread_scales = spread_bank[:].rearrange("p c i -> p (c i)")
        nc.scalar.copy(out=scale_tile[:, 0:D], in_=spread_scales)
        quantize(rbf_grouped[0][:], rbf_mx, group_cols(0))
        quantize(w_f_grouped[:, : F * QUAD // 2], w_f_mx, slice(0, F // 2))
        quantize(w_f_grouped[:, F * QUAD // 2 :], w_f_mx, slice(F // 2, F))
        bias_bank = new_bank([P, P], "bias_bank")
        nc.tensor.transpose(bias_bank[:], neg_bias_rows[:], ident[:])
        nc.scalar.copy(out=neg_bias[:], in_=bias_bank[:, : BLOCKS + 1])
        nc.gpsimd.tensor_scalar(out=ln2_bias[:], in0=neg_bias[:, :BLOCKS], scalar1=LN2, scalar2=None, op0=ALU.add)
        scale_x(0)
        for t in range(1, QUAD):
            nc.scalar.copy(out=scale_tile[:, t * D : (t + 1) * D], in_=spread_scales)
        b_a_bank = new_bank([P, S], "b_a_bank")
        nc.tensor.transpose(b_a_bank[:], neg_bias[:, BLOCKS : BLOCKS + 1].to_broadcast([P, P]), ident[:])

        w_h_raw = {}
        w_h_grouped = {}
        for s in range(GROUPS + 1):
            if s + 3 < GROUPS:
                load_rbf(s + 3)
                load_x(s + 3)
            if s == 2:
                w_h_raw[0] = load_weight(w_h, F)
            if s == 5:
                load_row_factor(occ_raw, occ)
                load_row_factor(cut_raw, cut)
                nc.gpsimd.tensor_scalar(out=neg_cut[:], in0=cut_raw[:], scalar1=-1.0, scalar2=None, op0=ALU.mult)
            if s < GROUPS:
                for c in range(BLOCKS):
                    sigmoid(s, c, filter_product(s, c))
            if s == 0:
                turn_rbf(1)
                w_a_grouped = work.tile([P, S * QUAD], BF16, name="w_a_grouped", tag="w_a_grouped", bufs=1, align_bytes=64)
                interleave_weight(-1.0, w_a_grouped[:], w_a_raw[:])
            if s > 0:
                quantize(x_grouped[s - 1][:], x_mx, group_cols(s - 1))
            if s > 1:
                slot_max(s - 2)
            if s < GROUPS:
                x_grouped[s] = new_grouped()
                x_banks = [turn(x_scaled[s], b) for b in range(2)]
                copy_turned(x_banks[0], x_grouped[s], 0, nc.scalar.copy)
                if s not in VECTOR_X_COPIES:
                    copy_turned(x_banks[1], x_grouped[s], 1, nc.scalar.copy)
            if s > 0:
                slot_product(s - 1)
            if s == 0:
                quantize_rbf(1)
                quantize(w_a_grouped[:], w_a_mx, slice(0, S))
                nc.vector.tensor_copy(out=neg_b_a[:], in_=b_a_bank[:])
            if s + 2 < GROUPS:
                turn_rbf(s + 2)
            if s + 1 < GROUPS:
                scale_x(s + 1)
            if s > 0:
                slot_bias(s - 1)
            if s in VECTOR_X_COPIES:
                copy_turned(x_banks[1], x_grouped[s], 1, nc.vector.tensor_copy)
            if s + 2 < GROUPS:
                quantize_rbf(s + 2)
            if s == W_H_STEP:
                w_h_grouped[0] = work.tile(
                    [P, F * QUAD], BF16, name="w_grouped", tag="w_grouped", bufs=1, align_bytes=64
                )
                nc.vector.tensor_copy(out=by_columns(w_h_grouped[0][:]), in_=by_rows(w_h_raw[0][:]))
            if s == W_H_STEP + 1:
                quantize(w_h_grouped[0][:], w_h_mx, slice(0, F))
        slot_max(GROUPS - 1)

        def logarithm(g, c0, c1):
            nc.scalar.activation(
                out=soft[:, g, c0:c1, :], in_=soft[:, g, c0:c1, :], func=ACT.Ln, bias=floor[:], scale=2.0
            )

        filter_bank = {}
        spread = {}

        def product_again(i):
            filter_bank[i] = filter_product(i // BLOCKS, i % BLOCKS)

        def minimum(i):
            g, c = divmod(i, BLOCKS)
            if c == 0:
                spread[g] = work.tile([P, BLOCKS, GROUP], F32, name="spread", tag="spread", bufs=2, align_bytes=64)
            nc.vector.scalar_tensor_tensor(
                out=spread[g][:, c, :],
                in0=filter_bank.pop(i)[:],
                scalar=ln2_bias[:, c : c + 1],
                in1=soft[:, g, c, :],
                op0=ALU.add,
                op1=ALU.min,
            )

        turned = {}
        late_banks = {}

        def turn_back(i):
            g, t0 = divmod(i, QUAD)
            if t0 == 0:
                turned[g] = work.tile([P, QUAD, F], F32, name="turned", tag="turned", bufs=2, align_bytes=64)
            banks = {}
            for t in range(t0, t0 + 2):
                banks[t] = new_bank([P, F], "back_bank")
                for c in range(BLOCKS):
                    nc.tensor.transpose(banks[t][:, block_cols(c)], spread[g][:, c, block_cols(t)], ident[:])
            for t in range(t0, t0 + 2):
                if QUAD * g + t in VECTOR_CUT_COPIES:
                    late_banks[g, t] = banks[t]
                else:
                    nc.scalar.activation(
                        out=turned[g][:, t, :], in_=banks[t][:], func=ACT.Copy, scale=neg_cut[:, g, t : t + 1]
                    )

        def late_copies():
            for g, t in sorted(late_banks):
                nc.vector.tensor_scalar(
                    out=turned[g][:, t, :],
                    in0=late_banks[g, t][:],
                    scalar1=neg_cut[:, g, t : t + 1],
                    scalar2=None,
                    op0=ALU.mult,
                )
            late_banks.clear()

        h_bank = {}
        m_grouped = {}

        def feature_product(i):
            g, c = divmod(i, BLOCKS)
            h_bank[i] = new_bank([P, QUAD, P], "feature_bank")
            for t in range(QUAD):
                mx_matmul(h_bank[i][:, t, :], x_mx, quad_cols(g, t), w_h_mx, block_cols(c))

        def message(i):
            g, c = divmod(i, BLOCKS)
            if c == 0:
                m_grouped[g] = new_grouped()
            nc.vector.tensor_tensor(
                out=by_columns(m_grouped[g][:, c * QUAD * P : (c + 1) * QUAD * P]),
                in0=by_rows(h_bank.pop(i)[:]),
                in1=by_rows(turned[g][:, :, block_cols(c)]),
                op=ALU.mult,
            )

        m_codes = {}
        m_mx = {}

        def open_environment(b):
            if b == 0:
                codes = work.tile([P, 4 * F], U32, name="m_codes_01", tag="scale_tile", bufs=1, align_bytes=64)
                m_codes[0] = codes[:, : 2 * F]
                m_codes[1] = codes[:, 2 * F :]
            if b == 2:
                codes = work.tile([P, 2 * F], U32, name="m_codes_2", tag="x_scaled", bufs=3, align_bytes=64)
                m_codes[2] = codes[:]
            if b == 3:
                codes = work.tile([P, 2 * F], U32, name="m_codes_3", tag="w_grouped", bufs=1, align_bytes=64)
                m_codes[3] = codes[:]
            m_bytes = work.tile([P, 2 * F], U8, name="m_bytes", tag="m_bytes", bufs=4, align_bytes=64)
            m_mx[b] = (m_codes[b], m_bytes)

        def quantize_m(g, f0, f1):
            b, half = divmod(g, 2)
            if half == 0:
                open_environment(b)
            quantize(m_grouped[g][:, f0 * QUAD : f1 * QUAD], m_mx[b], slice(half * F + f0, half * F + f1))

        def exponential(g):
            for t in range(QUAD):
                nc.scalar.activation(
                    out=z[:, g, t, :],
                    in_=z[:, g, t, :],
                    func=ACT.Exp,
                    bias=neg_max[:, g, t : t + 1],
                    scale=-1.0,
                    accum_out=exp_sum[:, g, t : t + 1],
                )

        def weight_inverse(g0):
            nc.vector.reciprocal(out=inverse[:, g0 : g0 + 2, :], in_=exp_sum[:, g0 : g0 + 2, :])

        def weight_factor(g0):
            nc.vector.scalar_tensor_tensor(
                out=factor[:, g0 : g0 + 2, :],
                in0=inverse[:, g0 : g0 + 2, :],
                scalar=float(S),
                in1=occ_raw[:, g0 : g0 + 2, :],
                op0=ALU.mult,
                op1=ALU.mult,
            )

        a_grouped = {}

        def weight_product(g0):
            for g in range(g0, g0 + 2):
                h, part = divmod(g, GROUPS // 2)
                if part == 0:
                    a_grouped[h] = work.tile(
                        [P, GROUPS // 2, S * QUAD], BF16, name="a_grouped", tag="x_scaled", bufs=3, align_bytes=64
                    )
                engine = nc.vector if g in VECTOR_WEIGHTS else nc.gpsimd
                engine.tensor_tensor(
                    out=by_columns(a_grouped[h][:, part, :]),
                    in0=by_rows(z[:, g, :, :]),
                    in1=factor[:, g, :].unsqueeze(1).unsqueeze(3).to_broadcast([P, S // RUN, QUAD, RUN]),
                    op=ALU.mult,
                )

        def quantize_a(h):
            cols = slice(h * GROUPS // 2 * S, (h + 1) * GROUPS // 2 * S)
            quantize(a_grouped[h][:].rearrange("p g n -> p (g n)"), a_mx, cols)

        def mix(b, f0, f1):
            bank = new_bank([P, F], "mix_bank")
            for half in range(2):
                g = 2 * b + half
                mx_matmul(
                    bank[:, : f1 - f0],
                    a_mx,
                    slice(g * S, (g + 1) * S),
                    m_mx[b],
                    slice(half * F + f0, half * F + f1),
                    start=(half == 0),
                    stop=(half == 1),
                )
            name = "y_%d" % (f1 - f0)
            y = work.tile([P, f1 - f0], F32, name=name, tag=name, bufs=2)
            nc.scalar.activation(out=y[:], in_=bank[:, : f1 - f0], func=ACT.Copy, scale=1.0 / math.sqrt(J))
            nc.sync.dma_start(out=out[b][:, f0:f1], in_=y[:])

        def do(step, item):
            if 0 <= item < ITEMS:
                step(item)

        logarithm(0, 0, BLOCKS // 2)
        logarithm(0, BLOCKS // 2, BLOCKS)
        product_again(0)
        product_again(1)
        logs = 1
        exps = 0
        summed = 0
        weighted = 0
        a_done = 0
        mixed = 0
        for n in range(ITEMS // 2 + 4):
            i = 2 * n
            g, c = divmod(i, BLOCKS)
            do(turn_back, i - 4)
            while logs < min(GROUPS, LN_LEAD + n * LN_RATE[0] // LN_RATE[1]):
                logarithm(logs, 0, BLOCKS)
                logs += 1
            while exps < min(GROUPS, (n - EXP_START) * EXP_RATE[0] // EXP_RATE[1]):
                exponential(exps)
                exps += 1
            weigh = weighted + 2 <= summed
            summed = exps
            do(minimum, i)
            if c == 0 and 0 <= g - 3 < GROUPS - 1:
                quantize_m(g - 3, 0, F)
            if weigh:
                weight_inverse(weighted)
            do(message, i - 8)
            do(product_again, i + 2)
            do(feature_product, i - 6)
            do(minimum, i + 1)
            if a_done < weighted // 4:
                quantize_a(a_done)
                a_done += 1
            if weigh:
                weight_factor(weighted)
            if n == ITEMS // 2 + 3:
                quantize_m(GROUPS - 1, 0, F // 2)
            late_copies()
            do(message, i - 7)
            do(product_again, i + 3)
            do(feature_product, i - 5)
            if weigh:
                weight_product(weighted)
                weighted += 2
            if mixed < min(B - 1, 2 * a_done) and 2 * mixed + 1 <= g - 3:
                mix(mixed, 0, F)
                mixed += 1
        while a_done < 2:
            quantize_a(a_done)
            a_done += 1
        while mixed < B - 1:
            mix(mixed, 0, F)
            mixed += 1
        quantize_m(GROUPS - 1, F // 2, 3 * F // 4)
        mix(B - 1, 0, F // 2)
        quantize_m(GROUPS - 1, 3 * F // 4, F)
        mix(B - 1, F // 2, 3 * F // 4)
        mix(B - 1, 3 * F // 4, F)
